import numpy as np
import ml_dtypes


def mxq(x, axis, fmt="e4m3"):
    dtype, down = {"e4m3": (ml_dtypes.float8_e4m3fn, 7), "e5m2": (ml_dtypes.float8_e5m2, 14)}[fmt]
    v = np.moveaxis(np.asarray(x, np.float32).astype(ml_dtypes.bfloat16).astype(np.float64), axis, -1)
    blocks = v.reshape(v.shape[:-1] + (-1, 32))
    amax = np.abs(blocks).max(-1, keepdims=True)
    byte = np.maximum(np.where(amax > 0, np.frexp(amax)[1] - 1 + 127, 0) - down, 1)
    scale = np.exp2(byte - 127.0)
    codes = (blocks / scale).astype(np.float32).astype(dtype).astype(np.float64)
    return np.moveaxis((codes * scale).reshape(v.shape), -1, axis)


WIDE = False


def mx_kscale(k):
    if not WIDE:
        return np.ones(k)
    levels = np.array([10, -10, 5, -5, 0])
    if k % 512:
        return np.exp2(np.random.permutation(np.resize(levels, k // 32))).repeat(32)
    a = np.empty((k // 512, 16))
    for p in range(k // 512):
        a[p, :8] = np.random.permutation(np.resize(levels, 8))
        for g in range(8):
            far = levels[np.abs(levels - a[p, g]) >= 10]
            a[p, g + 8] = far[np.random.randint(len(far))]
    return np.exp2(a.ravel()).repeat(32)


def f64(x):
    return np.asarray(x).astype(np.float64)


def striped(idx):
    return np.tile(idx.reshape(-1, 16).T, (8, 1)).astype(np.uint16)


def unstriped(offs):
    return offs[:16].T.reshape(-1).astype(np.int64)


E2M1 = np.array([0.0, 0.5, 1.0, 1.5, 2.0, 3.0, 4.0, 6.0, -0.0, -0.5, -1.0, -1.5, -2.0, -3.0, -4.0, -6.0])


def pack_weight(w, fmt):
    k, n = w.shape
    w = f64(np.asarray(w, np.float32).astype(ml_dtypes.bfloat16)).reshape(k // 32, 32, n)
    amax = np.abs(w).max(1)
    if fmt == "e4m3":
        byte = np.frexp(amax)[1] - 1 + 127 - 7
    else:
        mant, ex = np.frexp(amax / 6.0)
        byte = np.where(mant > 0.5, ex, ex - 1) + 127
    byte = np.clip(np.where(amax > 0, byte, 1), 1, 254)
    scaled = (w * np.exp2(127.0 - byte)[:, None, :]).reshape(k, n).astype(np.float32)
    by_word = np.ascontiguousarray(scaled.reshape(k // 512, 128, 4, n).transpose(0, 1, 3, 2))
    if fmt == "e4m3":
        words = by_word.astype(ml_dtypes.float8_e4m3fn).view(np.uint8)
    else:
        c = by_word.astype(ml_dtypes.float4_e2m1fn).view(np.uint8) & 0xF
        words = (c[..., 0::2] | (c[..., 1::2] << 4)).reshape(k // 512, 128, 2 * n)
    return np.ascontiguousarray(words), np.ascontiguousarray(byte.astype(np.uint8).reshape(k // 512, 16, n))


def unpack_weight(words, scales, fmt):
    g, _, n = scales.shape
    words = np.ascontiguousarray(words).reshape(g, 128, n, -1)
    if fmt == "e4m3":
        vals = words.view(ml_dtypes.float8_e4m3fn).astype(np.float64)
    else:
        nib = np.empty((g, 128, n, 4), np.uint8)
        nib[..., 0::2] = words & 0xF
        nib[..., 1::2] = words >> 4
        vals = E2M1[nib]
    vals = vals * np.repeat(np.exp2(scales.astype(np.float64) - 127.0), 8, axis=1)[..., None]
    return vals.transpose(0, 1, 3, 2).reshape(g * 512, n)


def gelu(v):
    return 0.5 * v * (1.0 + np.tanh(np.sqrt(2.0 / np.pi) * (v + 0.044715 * v**3)))


K, H, N, T, S = 1536, 1024, 768, 4096, 1024

def setup_inputs():
    n = np.random.standard_normal
    s = mx_kscale(K)[:, None]
    u = mx_kscale(H)[:, None]
    tab_words, tab_scales = pack_weight(n((K, T)) * s, "e4m3")
    w1_words, w1_scales = pack_weight(0.6 * n((K, H)) / np.sqrt(K) / s, "e2m1")
    return {
        "tab_words": tab_words, "tab_scales": tab_scales,
        "offs": striped(np.random.permutation(T)[:S]),
        "w1_words": w1_words, "w1_scales": w1_scales,
        "comp": (0.6 * np.exp(0.7 * n((H, S)))).astype(np.float32),
        "cap": (1.5 * np.exp(0.3 * n(H)) * u[:, 0]).astype(np.float32),
        "w2": (n((H, N)) / np.sqrt(H) / u).astype(np.float32),
        "offs2": striped(np.random.permutation(S)),
        "wgo": np.exp(0.3 * n((128, S))).astype(np.float32),
        "x0": n((N, S)).astype(np.float32),
    }

def reference(tab_words, tab_scales, offs, w1_words, w1_scales, comp, cap, w2, offs2, wgo, x0):
    v = unpack_weight(tab_words, tab_scales, "e4m3")[:, unstriped(offs)]
    w1 = unpack_weight(w1_words, w1_scales, "e2m1")
    a = w1.T @ v
    d = np.exp(a) + f64(comp)
    h = f64(cap)[:, None] * (1.0 / d)
    y = mxq(f64(w2), 0, "e4m3").T @ mxq(h, 0, "e4m3")
    page = np.zeros((N, S))
    page[:, unstriped(offs2)] = np.tile(f64(wgo), (N // 128, 1)) * y
    x = f64(x0)
    return page * x + x

@@ -1,0 +1,304 @@
+from contextlib import ExitStack
+
+import concourse.mybir as mybir
+from concourse.masks import make_identity
+
+K, H, N, T, S = 1536, 1024, 768, 4096, 1024
+FLOPS = 2 * K * H * S + 2 * H * N * S
+
+F32 = mybir.dt.float32
+BF16 = mybir.dt.bfloat16
+I32 = mybir.dt.int32
+U32 = mybir.dt.uint32
+U16 = mybir.dt.uint16
+U8 = mybir.dt.uint8
+FP8X4 = mybir.dt.float8_e4m3fn_x4
+FP4X4 = mybir.dt.float4_e2m1fn_x4
+ACT = mybir.ActivationFunctionType
+ALU = mybir.AluOpType
+
+P = 128
+PACK = 4
+BANK = 512
+K_PASSES = K // (P * PACK)
+H_PASSES = H // (P * PACK)
+R_TILES = H // P
+N_TILES = N // P
+HALF = 512
+SUB = 128
+SUBS_PER_HALF = HALF // SUB
+W2_COLS = 256
+Y_TILES = 3
+SCALE_ROW0 = 16
+
+
+def tile_list_fraction_loading_kernel(
+    tc, tab_words, tab_scales, offs, w1_words, w1_scales, comp, cap, w2, offs2, wgo, x0, out
+):
+    nc = tc.nc
+    with ExitStack() as ctx:
+        keep = ctx.enter_context(tc.tile_pool(name="keep", bufs=1))
+        ring = ctx.enter_context(tc.tile_pool(name="ring", bufs=2))
+        psum = ctx.enter_context(tc.psum_pool(name="psum", bufs=1))
+
+        def bank(b):
+            return psum.tile([P, BANK], F32, name="bank%d" % b, tag="bank%d" % b)
+
+        table = [ring.tile([P, T], U32, name="table%d" % a, tag="big", bufs=K_PASSES) for a in range(K_PASSES)]
+        idx = keep.tile([P, S // 16], U16, name="idx")
+        idx2 = keep.tile([P, S // 16], U16, name="idx2")
+        w1c = keep.tile([P, K_PASSES, 2 * H], U8, name="w1c", align_bytes=64)
+        w1s = keep.tile([P, K_PASSES, H], U8, name="w1s", align_bytes=64)
+        tscale = keep.tile([P, T], U8, name="tscale")
+        capt = keep.tile([P, R_TILES], F32, name="capt")
+
+        def load_table(a):
+            nc.sync.dma_start(table[a][:].bitcast(I32), tab_words[a].rearrange("p t i -> p (t i)").bitcast(I32))
+
+        load_table(0)
+        nc.sync.dma_start(idx[:], offs)
+        nc.scalar.dma_start(
+            tscale[SCALE_ROW0 : SCALE_ROW0 + 16 * K_PASSES, :].bitcast(I32),
+            tab_scales.rearrange("a q t -> (a q) t").bitcast(I32),
+        )
+        with nc.allow_non_contiguous_dma(reason="one gain a partition"):
+            nc.scalar.dma_start(capt[:], cap.rearrange("(c p) -> p c", p=P))
+        nc.sync.dma_start(w1c[:].bitcast(I32), w1_words.rearrange("a p n -> p a n").bitcast(I32))
+        load_table(1)
+        load_table(2)
+        nc.sync.dma_start(idx2[:], offs2)
+
+        nc.vector.memset(tscale[0:SCALE_ROW0, :].bitcast(I32), 0)
+        nc.vector.memset(tscale[64:P, :].bitcast(I32), 0)
+        nc.vector.memset(w1s[:].bitcast(I32), 0)
+        for q in range(4):
+            nc.gpsimd.dma_start(
+                w1s[32 * q : 32 * q + 4, :, :].bitcast(I32),
+                w1_scales[:, 4 * q : 4 * q + 4, :].rearrange("a r n -> r a n").bitcast(I32),
+            )
+        vs = [keep.tile([P, S], U8, name="vs%d" % a, align_bytes=64) for a in range(K_PASSES)]
+        for a in range(K_PASSES):
+            nc.vector.memset(vs[a][:].bitcast(I32), 0)
+        ident = keep.tile([P, P], F32, name="ident")
+        make_identity(nc, ident[:])
+
+        compt = {}
+
+        def load_comp(h):
+            for g in range(H_PASSES):
+                compt[h, g] = keep.tile([P, PACK, HALF], F32, name="comp%d_%d" % (h, g))
+                nc.sync.dma_start(
+                    compt[h, g][:],
+                    comp[g * 512 : (g + 1) * 512, h * HALF : (h + 1) * HALF].rearrange("(c p) j -> p c j", p=P),
+                )
+
+        load_comp(0)
+        w2raw = {}
+        wgot = keep.tile([P, S], F32, name="wgot")
+        for c in range(N // W2_COLS):
+            for g in range(H_PASSES):
+                w2raw[c, g] = keep.tile([P, PACK, W2_COLS], F32, name="w2raw%d_%d" % (c, g))
+                nc.sync.dma_start(
+                    w2raw[c, g][:],
+                    w2[g * 512 : (g + 1) * 512, c * W2_COLS : (c + 1) * W2_COLS].rearrange("(p t) n -> p t n", t=PACK),
+                )
+            if c == 1:
+                nc.sync.dma_start(wgot[:], wgo)
+        load_comp(1)
+
+        lncap = keep.tile([P, R_TILES], F32, name="lncap")
+        nlncap = keep.tile([P, R_TILES], F32, name="nlncap")
+        rcap = keep.tile([P, R_TILES], F32, name="rcap")
+        nc.scalar.activation(lncap[:], capt[:], ACT.Ln)
+        nc.scalar.activation(rcap[:], lncap[:], ACT.Exp, scale=-1.0)
+        nc.vector.tensor_scalar(nlncap[:], lncap[:], -1.0, None, ALU.mult)
+
+        gscale = keep.tile([P, S], U8, name="gscale")
+        nc.vector.tensor_copy(gscale[:], tscale[:].indirect(idx[:]))
+        for a in range(K_PASSES):
+            for q in range(4):
+                r0 = SCALE_ROW0 + 16 * a + 4 * q
+                nc.gpsimd.dma_start(vs[a][32 * q : 32 * q + 4, :].bitcast(I32), gscale[r0 : r0 + 4, :].bitcast(I32))
+        vc = {}
+        for a in range(K_PASSES - 1):
+            whole = keep.tile([P, S], U32, name="vc%d" % a, align_bytes=64)
+            nc.vector.tensor_copy(whole[:], table[a][:].indirect(idx[:]))
+            for h in range(2):
+                vc[a, h] = whole[:, h * HALF : (h + 1) * HALF]
+        a = K_PASSES - 1
+        for h in range(2):
+            part = keep.tile([P, HALF], U32, name="vc%d_%d" % (a, h), align_bytes=64)
+            nc.vector.tensor_copy(part[:], table[a][:].indirect(idx[:, h * HALF // 16 : (h + 1) * HALF // 16]))
+            vc[a, h] = part[:]
+
+        xt = []
+        for c in range(N_TILES // 2):
+            pair = ring.tile([P, 2, S], F32, name="x%d" % c, tag="big", bufs=K_PASSES)
+            nc.sync.dma_start(pair[:], x0[2 * c * P : (2 * c + 2) * P, :].rearrange("(c p) m -> p c m", p=P))
+            xt.extend([pair[:, 0, :], pair[:, 1, :]])
+
+        state = {}
+
+        def mm1_pass(h, rt, a, acc):
+            nc.tensor.matmul_mx(
+                out=acc[:],
+                lhsT=w1c[:, a, 2 * P * rt : 2 * P * (rt + 1)].bitcast(FP4X4),
+                lhsT_scale=w1s[:, a, P * rt : P * (rt + 1)],
+                rhs=vc[a, h].bitcast(FP8X4),
+                rhs_scale=vs[a][:, h * HALF : (h + 1) * HALF],
+                start=(a == 0),
+                stop=(a == K_PASSES - 1),
+            )
+
+        def new_work(h):
+            state["work", h] = ring.tile([P, SUBS_PER_HALF, R_TILES, SUB], F32, name="work%d" % h, tag="work", bufs=1)
+
+        def expo(h, rt, acc):
+            nc.scalar.activation(
+                state["work", h][:, :, rt, :],
+                acc[:].rearrange("p (s j) -> p s j", j=SUB),
+                ACT.Exp,
+                bias=nlncap[:, rt : rt + 1],
+            )
+
+        def prescale_vector(h, cols):
+            for rt in range(R_TILES):
+                t = compt[h, rt // PACK][:, rt % PACK, cols]
+                nc.vector.tensor_scalar(t, t, rcap[:, rt : rt + 1], None, ALU.mult)
+
+        def prescale_scalar(h, cols):
+            for rt in range(R_TILES):
+                t = compt[h, rt // PACK][:, rt % PACK, cols]
+                nc.scalar.activation(t, t, ACT.Copy, scale=rcap[:, rt : rt + 1])
+
+        def make_h(s):
+            h, sl = divmod(s, SUBS_PER_HALF)
+            work = state["work", h]
+            cols = slice(sl * SUB, (sl + 1) * SUB)
+            dts = []
+            for g in range(H_PASSES):
+                dt = bank(2 * ((s + h) % 2) + g)
+                for c in range(PACK):
+                    o = dt[:, c * P : (c + 1) * P]
+                    nc.tensor.matmul(o, compt[h, g][:, c, cols], ident[:], start=True, stop=False, is_transpose=True)
+                    nc.tensor.matmul(o, work[:, sl, g * PACK + c, :], ident[:], start=False, stop=True, is_transpose=True)
+                dts.append(dt)
+            for g in range(H_PASSES):
+                nc.scalar.activation(
+                    work[:, sl, g * PACK : (g + 1) * PACK, :],
+                    dts[g][:].rearrange("j (p t) -> j t p", t=PACK),
+                    ACT.Abs_reciprocal_sqrt,
+                )
+
+        def finish_h(s):
+            h, sl = divmod(s, SUBS_PER_HALF)
+            work = state["work", h]
+            hb = ring.tile([P, H_PASSES * SUB * PACK], BF16, name="hb", tag="hb", align_bytes=64)
+            for g in range(H_PASSES):
+                bk = bank(4 + g)
+                for t in range(PACK):
+                    nc.tensor.transpose(bk[:, t * SUB : (t + 1) * SUB], work[:, sl, g * PACK + t, :], ident[:])
+                nc.scalar.activation(
+                    hb[:, g * BANK : (g + 1) * BANK].rearrange("p (j t) -> p j t", t=PACK),
+                    bk[:].rearrange("p (t j) -> p j t", t=PACK),
+                    ACT.Square,
+                )
+            hc = ring.tile([P, H_PASSES * SUB], U32, name="hc", tag="hc", bufs=4, align_bytes=64)
+            hs = ring.tile([P, H_PASSES * SUB], U8, name="hs", tag="hs", bufs=4, align_bytes=64)
+            nc.vector.quantize_mx(out=hc[:].bitcast(FP8X4), scales=hs[:], in_=hb[:])
+            state["hq", s] = (hc, hs)
+
+        w2c, w2s = [], []
+
+        def quantize_w2(c):
+            w2b = ring.tile([P, H_PASSES * W2_COLS * PACK], BF16, name="w2b", tag="w2b", align_bytes=64)
+            for g in range(H_PASSES):
+                nc.vector.tensor_copy(
+                    w2b[:, g * W2_COLS * PACK : (g + 1) * W2_COLS * PACK].rearrange("p (c i t) -> p c t i", i=4, t=PACK),
+                    w2raw[c, g][:].rearrange("p t (c i) -> p c t i", i=4),
+                )
+            codes = keep.tile([P, H_PASSES * W2_COLS], U32, name="w2c%d" % c, align_bytes=64)
+            scales = keep.tile([P, H_PASSES * W2_COLS], U8, name="w2s%d" % c, align_bytes=64)
+            nc.vector.quantize_mx(out=codes[:].bitcast(FP8X4), scales=scales[:], in_=w2b[:])
+            w2c.append(codes)
+            w2s.append(scales)
+
+        pages = [keep.tile([P, S], F32, name="page%d" % nt) for nt in range(N_TILES)]
+
+        def finish_out(nt):
+            nc.vector.scalar_tensor_tensor(xt[nt], pages[nt][:], 1.0, xt[nt], ALU.add, ALU.mult)
+            nc.sync.dma_start(out[nt * P : (nt + 1) * P, :], xt[nt])
+
+        def place(s, part):
+            hc, hs = state["hq", s]
+            acc = bank(6 + part)
+            for i in range(Y_TILES):
+                nt = part * Y_TILES + i
+                c, off = divmod(nt * P, W2_COLS)
+                for g in range(H_PASSES):
+                    w = slice(g * W2_COLS + off, g * W2_COLS + off + P)
+                    nc.tensor.matmul_mx(
+                        out=acc[:, i * SUB : (i + 1) * SUB],
+                        lhsT=w2c[c][:, w].bitcast(FP8X4),
+                        lhsT_scale=w2s[c][:, w],
+                        rhs=hc[:, g * SUB : (g + 1) * SUB].bitcast(FP8X4),
+                        rhs_scale=hs[:, g * SUB : (g + 1) * SUB],
+                        start=(g == 0),
+                        stop=(g == H_PASSES - 1),
+                    )
+            y = ring.tile([P, Y_TILES * SUB], F32, name="y", tag="y", bufs=8)
+            nc.scalar.copy(y[:], acc[:, : Y_TILES * SUB])
+            for i in range(Y_TILES):
+                nt = part * Y_TILES + i
+                nc.vector.tensor_tensor(
+                    pages[nt][:].indirect(idx2[:, s * SUB // 16 : (s + 1) * SUB // 16]),
+                    y[:, i * SUB : (i + 1) * SUB],
+                    wgot[:, s * SUB : (s + 1) * SUB],
+                    ALU.mult,
+                )
+                if s == S // SUB - 1 and nt > 0:
+                    finish_out(nt - 1)
+
+        accs = [bank(rt) for rt in range(R_TILES)]
+        for a in range(K_PASSES):
+            for rt in range(R_TILES):
+                mm1_pass(0, rt, a, accs[rt])
+        new_work(0)
+        for rt in range(R_TILES):
+            expo(0, rt, accs[rt])
+        prescale_vector(0, slice(0, HALF))
+        quantize_w2(0)
+        quantize_w2(1)
+        make_h(0)
+        finish_h(0)
+        quantize_w2(2)
+        make_h(1)
+        place(0, 0)
+        finish_h(1)
+        place(0, 1)
+        for s in (1, 2):
+            make_h(s + 1)
+            finish_h(s + 1)
+            place(s, 0)
+            place(s, 1)
+        new_work(1)
+        for rt in range(R_TILES):
+            acc = bank(rt % 6)
+            for a in range(K_PASSES):
+                mm1_pass(1, rt, a, acc)
+            expo(1, rt, acc)
+            if rt == 3:
+                place(3, 0)
+        prescale_vector(1, slice(0, SUB))
+        make_h(4)
+        finish_h(4)
+        place(3, 1)
+        prescale_scalar(1, slice(SUB, HALF))
+        for s in (4, 5, 6):
+            make_h(s + 1)
+            finish_h(s + 1)
+            place(s, 0)
+            place(s, 1)
+        place(7, 0)
+        place(7, 1)
+        finish_out(N_TILES - 1)

@@ -47,38 +47,49 @@ def tile_list_fraction_loading_kernel(
         table = [ring.tile([P, T], U32, name="table%d" % a, tag="big", bufs=K_PASSES) for a in range(K_PASSES)]
         idx = keep.tile([P, S // 16], U16, name="idx")
         idx2 = keep.tile([P, S // 16], U16, name="idx2")
-        w1c = keep.tile([P, K_PASSES, 2 * H], U8, name="w1c", align_bytes=64)
+        w1first = keep.tile([P, K_PASSES - 1, 2 * H], U8, name="w1first", align_bytes=64)
+        w1last = keep.tile([P, 2 * H], U8, name="w1last", align_bytes=64)
+        w1c = [w1first[:, a, :] for a in range(K_PASSES - 1)] + [w1last[:]]
         w1s = keep.tile([P, K_PASSES, H], U8, name="w1s", align_bytes=64)
         tscale = keep.tile([P, T], U8, name="tscale")
-        capt = keep.tile([P, R_TILES], F32, name="capt")
+        caprows = keep.tile([P, P], F32, name="caprows")
 
         def load_table(a):
             nc.sync.dma_start(table[a][:].bitcast(I32), tab_words[a].rearrange("p t i -> p (t i)").bitcast(I32))
 
-        load_table(0)
-        nc.sync.dma_start(idx[:], offs)
-        nc.scalar.dma_start(
-            tscale[SCALE_ROW0 : SCALE_ROW0 + 16 * K_PASSES, :].bitcast(I32),
-            tab_scales.rearrange("a q t -> (a q) t").bitcast(I32),
-        )
-        with nc.allow_non_contiguous_dma(reason="one gain a partition"):
-            nc.scalar.dma_start(capt[:], cap.rearrange("(c p) -> p c", p=P))
-        nc.sync.dma_start(w1c[:].bitcast(I32), w1_words.rearrange("a p n -> p a n").bitcast(I32))
-        load_table(1)
-        load_table(2)
-        nc.sync.dma_start(idx2[:], offs2)
-
+        vs = keep.tile([P, K_PASSES, S], U8, name="vs", align_bytes=64)
+        nc.vector.memset(w1s[:].bitcast(I32), 0)
         nc.vector.memset(tscale[0:SCALE_ROW0, :].bitcast(I32), 0)
         nc.vector.memset(tscale[64:P, :].bitcast(I32), 0)
-        nc.vector.memset(w1s[:].bitcast(I32), 0)
+        nc.vector.memset(vs[:].bitcast(I32), 0)
+
+        nc.sync.dma_start(idx[:], offs)
+        nc.sync.dma_start(
+            tscale[SCALE_ROW0 : SCALE_ROW0 + 16 * K_PASSES, :].bitcast(I32),
+            tab_scales.rearrange("a q t -> q a t").bitcast(I32),
+        )
+        load_table(0)
         for q in range(4):
-            nc.gpsimd.dma_start(
+            nc.sync.dma_start(
                 w1s[32 * q : 32 * q + 4, :, :].bitcast(I32),
                 w1_scales[:, 4 * q : 4 * q + 4, :].rearrange("a r n -> r a n").bitcast(I32),
             )
-        vs = [keep.tile([P, S], U8, name="vs%d" % a, align_bytes=64) for a in range(K_PASSES)]
-        for a in range(K_PASSES):
-            nc.vector.memset(vs[a][:].bitcast(I32), 0)
+        nc.gpsimd.memset(caprows[:], 0.0)
+        nc.scalar.dma_start(caprows[0:R_TILES, :], cap.rearrange("(c p) -> c p", p=P))
+        nc.sync.dma_start(
+            w1first[:].bitcast(I32), w1_words[0 : K_PASSES - 1].rearrange("a p n -> p a n").bitcast(I32)
+        )
+        load_table(1)
+        gscale = keep.tile([P, S], U8, name="gscale")
+        nc.vector.tensor_copy(gscale[:], tscale[:].indirect(idx[:]))
+        for q in range(4):
+            r0 = SCALE_ROW0 + 4 * K_PASSES * q
+            nc.scalar.dma_start(
+                vs[32 * q : 32 * q + 4, :, :].bitcast(I32), gscale[r0 : r0 + 4 * K_PASSES, :].bitcast(I32)
+            )
+        load_table(2)
+        nc.sync.dma_start(w1last[:].bitcast(I32), w1_words[K_PASSES - 1].bitcast(I32))
+        nc.sync.dma_start(idx2[:], offs2)
         ident = keep.tile([P, P], F32, name="ident")
         make_identity(nc, ident[:])
 
@@ -109,16 +120,12 @@ def tile_list_fraction_loading_kernel(
         lncap = keep.tile([P, R_TILES], F32, name="lncap")
         nlncap = keep.tile([P, R_TILES], F32, name="nlncap")
         rcap = keep.tile([P, R_TILES], F32, name="rcap")
-        nc.scalar.activation(lncap[:], capt[:], ACT.Ln)
+        capt = bank(7)
+        nc.tensor.transpose(capt[:, :P], caprows[:], ident[:])
+        nc.scalar.activation(lncap[:], capt[:, :R_TILES], ACT.Ln)
         nc.scalar.activation(rcap[:], lncap[:], ACT.Exp, scale=-1.0)
         nc.vector.tensor_scalar(nlncap[:], lncap[:], -1.0, None, ALU.mult)
 
-        gscale = keep.tile([P, S], U8, name="gscale")
-        nc.vector.tensor_copy(gscale[:], tscale[:].indirect(idx[:]))
-        for a in range(K_PASSES):
-            for q in range(4):
-                r0 = SCALE_ROW0 + 16 * a + 4 * q
-                nc.gpsimd.dma_start(vs[a][32 * q : 32 * q + 4, :].bitcast(I32), gscale[r0 : r0 + 4, :].bitcast(I32))
         vc = {}
         for a in range(K_PASSES - 1):
             whole = keep.tile([P, S], U32, name="vc%d" % a, align_bytes=64)
@@ -142,10 +149,10 @@ def tile_list_fraction_loading_kernel(
         def mm1_pass(h, rt, a, acc):
             nc.tensor.matmul_mx(
                 out=acc[:],
-                lhsT=w1c[:, a, 2 * P * rt : 2 * P * (rt + 1)].bitcast(FP4X4),
+                lhsT=w1c[a][:, 2 * P * rt : 2 * P * (rt + 1)].bitcast(FP4X4),
                 lhsT_scale=w1s[:, a, P * rt : P * (rt + 1)],
                 rhs=vc[a, h].bitcast(FP8X4),
-                rhs_scale=vs[a][:, h * HALF : (h + 1) * HALF],
+                rhs_scale=vs[:, a, h * HALF : (h + 1) * HALF],
                 start=(a == 0),
                 stop=(a == K_PASSES - 1),
             )
@@ -171,13 +178,13 @@ def tile_list_fraction_loading_kernel(
                 t = compt[h, rt // PACK][:, rt % PACK, cols]
                 nc.scalar.activation(t, t, ACT.Copy, scale=rcap[:, rt : rt + 1])
 
-        def make_h(s):
+        def make_h(s, banks):
             h, sl = divmod(s, SUBS_PER_HALF)
             work = state["work", h]
             cols = slice(sl * SUB, (sl + 1) * SUB)
             dts = []
             for g in range(H_PASSES):
-                dt = bank(2 * ((s + h) % 2) + g)
+                dt = bank(banks[g])
                 for c in range(PACK):
                     o = dt[:, c * P : (c + 1) * P]
                     nc.tensor.matmul(o, compt[h, g][:, c, cols], ident[:], start=True, stop=False, is_transpose=True)
@@ -190,12 +197,12 @@ def tile_list_fraction_loading_kernel(
                     ACT.Abs_reciprocal_sqrt,
                 )
 
-        def finish_h(s):
+        def finish_h(s, banks):
             h, sl = divmod(s, SUBS_PER_HALF)
             work = state["work", h]
             hb = ring.tile([P, H_PASSES * SUB * PACK], BF16, name="hb", tag="hb", align_bytes=64)
             for g in range(H_PASSES):
-                bk = bank(4 + g)
+                bk = bank(banks[g])
                 for t in range(PACK):
                     nc.tensor.transpose(bk[:, t * SUB : (t + 1) * SUB], work[:, sl, g * PACK + t, :], ident[:])
                 nc.scalar.activation(
@@ -225,13 +232,15 @@ def tile_list_fraction_loading_kernel(
 
         pages = [keep.tile([P, S], F32, name="page%d" % nt) for nt in range(N_TILES)]
 
-        def finish_out(nt):
-            nc.vector.scalar_tensor_tensor(xt[nt], pages[nt][:], 1.0, xt[nt], ALU.add, ALU.mult)
-            nc.sync.dma_start(out[nt * P : (nt + 1) * P, :], xt[nt])
+        def finish_out(nt, pieces=1):
+            for i in range(pieces):
+                m = slice(i * S // pieces, (i + 1) * S // pieces)
+                nc.vector.scalar_tensor_tensor(xt[nt][:, m], pages[nt][:, m], 1.0, xt[nt][:, m], ALU.add, ALU.mult)
+                nc.sync.dma_start(out[nt * P : (nt + 1) * P, m], xt[nt][:, m])
 
-        def place(s, part):
+        def place(s, part, b):
             hc, hs = state["hq", s]
-            acc = bank(6 + part)
+            acc = bank(b)
             for i in range(Y_TILES):
                 nt = part * Y_TILES + i
                 c, off = divmod(nt * P, W2_COLS)
@@ -269,36 +278,47 @@ def tile_list_fraction_loading_kernel(
         prescale_vector(0, slice(0, HALF))
         quantize_w2(0)
         quantize_w2(1)
-        make_h(0)
-        finish_h(0)
+        make_h(0, (0, 1))
+        finish_h(0, (4, 5))
         quantize_w2(2)
-        make_h(1)
-        place(0, 0)
-        finish_h(1)
-        place(0, 1)
-        for s in (1, 2):
-            make_h(s + 1)
-            finish_h(s + 1)
-            place(s, 0)
-            place(s, 1)
+        make_h(1, (2, 3))
+        place(0, 0, 6)
+        finish_h(1, (7, 4))
+        place(0, 1, 7)
+        make_h(2, (0, 1))
+        finish_h(2, (5, 6))
+        place(1, 0, 5)
+        make_h(3, (2, 3))
+        finish_h(3, (4, 7))
+        place(1, 1, 4)
+        place(2, 0, 7)
         new_work(1)
-        for rt in range(R_TILES):
-            acc = bank(rt % 6)
+        prescale_vector(1, slice(0, 2 * SUB))
+        for rt, b in enumerate((0, 1, 2, 3, 6, 5, 0, 1)):
+            acc = bank(b)
             for a in range(K_PASSES):
                 mm1_pass(1, rt, a, acc)
             expo(1, rt, acc)
-            if rt == 3:
-                place(3, 0)
-        prescale_vector(1, slice(0, SUB))
-        make_h(4)
-        finish_h(4)
-        place(3, 1)
-        prescale_scalar(1, slice(SUB, HALF))
-        for s in (4, 5, 6):
-            make_h(s + 1)
-            finish_h(s + 1)
-            place(s, 0)
-            place(s, 1)
-        place(7, 0)
-        place(7, 1)
-        finish_out(N_TILES - 1)
+            if rt == 2:
+                place(2, 1, 2)
+            if rt == 5:
+                place(3, 0, 6)
+        make_h(4, (4, 7))
+        finish_h(4, (0, 1))
+        place(3, 1, 0)
+        make_h(5, (3, 2))
+        place(4, 0, 5)
+        finish_h(5, (6, 1))
+        place(4, 1, 6)
+        prescale_scalar(1, slice(2 * SUB, HALF))
+        make_h(6, (4, 7))
+        finish_h(6, (0, 5))
+        place(5, 0, 0)
+        make_h(7, (3, 2))
+        finish_h(7, (1, 6))
+        place(5, 1, 1)
+        place(6, 0, 6)
+        place(6, 1, 3)
+        place(7, 0, 4)
+        place(7, 1, 7)
+        finish_out(N_TILES - 1, 2)

@@ -1,7 +1,6 @@
 from contextlib import ExitStack
 
 import concourse.mybir as mybir
-from concourse.masks import make_identity
 
 K, H, N, T, S = 1536, 1024, 768, 4096, 1024
 FLOPS = 2 * K * H * S + 2 * H * N * S
@@ -26,9 +25,10 @@ R_TILES = H // P
 N_TILES = N // P
 HALF = 512
 SUB = 128
+QUARTER = 256
 SUBS_PER_HALF = HALF // SUB
-W2_COLS = 256
 Y_TILES = 3
+W2_COLS = Y_TILES * P
 SCALE_ROW0 = 16
 
 
@@ -44,87 +44,94 @@ def tile_list_fraction_loading_kernel(
         def bank(b):
             return psum.tile([P, BANK], F32, name="bank%d" % b, tag="bank%d" % b)
 
-        table = [ring.tile([P, T], U32, name="table%d" % a, tag="big", bufs=K_PASSES) for a in range(K_PASSES)]
         idx = keep.tile([P, S // 16], U16, name="idx")
         idx2 = keep.tile([P, S // 16], U16, name="idx2")
-        w1first = keep.tile([P, K_PASSES - 1, 2 * H], U8, name="w1first", align_bytes=64)
-        w1last = keep.tile([P, 2 * H], U8, name="w1last", align_bytes=64)
-        w1c = [w1first[:, a, :] for a in range(K_PASSES - 1)] + [w1last[:]]
-        w1s = keep.tile([P, K_PASSES, H], U8, name="w1s", align_bytes=64)
-        tscale = keep.tile([P, T], U8, name="tscale")
-        caprows = keep.tile([P, P], F32, name="caprows")
+        w1raw = ring.tile([P, K_PASSES, H], U16, name="w1raw", tag="work", bufs=1)
+        w1sraw = ring.tile([P, K_PASSES, H], U8, name="w1sraw", tag="w2b", bufs=1, align_bytes=64)
+        capt = keep.tile([P, H_PASSES, PACK], F32, name="capt")
+        vs = keep.tile([P, K_PASSES, S], U8, name="vs", align_bytes=64)
+        gscale = keep.tile([P, S], U8, name="gscale")
+        table = []
 
-        def load_table(a):
+        def big_tile(pool, i, shape, dtype):
+            return pool.tile(shape, dtype, name="big%d" % i, tag="big%d" % i, bufs=1)
+
+        def load_table(pool, a):
+            table.append(big_tile(pool, a, [P, T], U32))
             nc.sync.dma_start(table[a][:].bitcast(I32), tab_words[a].rearrange("p t i -> p (t i)").bitcast(I32))
 
-        vs = keep.tile([P, K_PASSES, S], U8, name="vs", align_bytes=64)
-        nc.vector.memset(w1s[:].bitcast(I32), 0)
-        nc.vector.memset(tscale[0:SCALE_ROW0, :].bitcast(I32), 0)
-        nc.vector.memset(tscale[64:P, :].bitcast(I32), 0)
-        nc.vector.memset(vs[:].bitcast(I32), 0)
+        with tc.tile_pool(name="early", bufs=1) as early:
+            tscale = early.tile([P, T], U8, name="tscale")
+            nc.vector.memset(w1sraw[:].bitcast(I32), 0)
+            nc.vector.memset(tscale[0:SCALE_ROW0, :].bitcast(I32), 0)
+            nc.vector.memset(tscale[64:P, :].bitcast(I32), 0)
+            nc.vector.memset(vs[:].bitcast(I32), 0)
 
-        nc.sync.dma_start(idx[:], offs)
-        nc.sync.dma_start(
-            tscale[SCALE_ROW0 : SCALE_ROW0 + 16 * K_PASSES, :].bitcast(I32),
-            tab_scales.rearrange("a q t -> q a t").bitcast(I32),
-        )
-        load_table(0)
-        for q in range(4):
+            nc.sync.dma_start(idx[:], offs)
             nc.sync.dma_start(
-                w1s[32 * q : 32 * q + 4, :, :].bitcast(I32),
-                w1_scales[:, 4 * q : 4 * q + 4, :].rearrange("a r n -> r a n").bitcast(I32),
+                tscale[SCALE_ROW0 : SCALE_ROW0 + 16 * K_PASSES, :].bitcast(I32),
+                tab_scales.rearrange("a q t -> q a t").bitcast(I32),
             )
-        nc.gpsimd.memset(caprows[:], 0.0)
-        nc.scalar.dma_start(caprows[0:R_TILES, :], cap.rearrange("(c p) -> c p", p=P))
-        nc.sync.dma_start(
-            w1first[:].bitcast(I32), w1_words[0 : K_PASSES - 1].rearrange("a p n -> p a n").bitcast(I32)
-        )
-        load_table(1)
-        gscale = keep.tile([P, S], U8, name="gscale")
-        nc.vector.tensor_copy(gscale[:], tscale[:].indirect(idx[:]))
+            nc.sync.dma_start(idx2[:], offs2)
+            nc.sync.dma_start(w1raw[:].bitcast(I32), w1_words.rearrange("a p n -> p a n").bitcast(I32))
+            for q in range(4):
+                nc.sync.dma_start(
+                    w1sraw[32 * q : 32 * q + 4, :, :].bitcast(I32),
+                    w1_scales[:, 4 * q : 4 * q + 4, :].rearrange("a r n -> r a n").bitcast(I32),
+                )
+            load_table(ring, 0)
+            nc.gpsimd.dma_start(capt[:], cap.rearrange("(g p t) -> p g t", p=P, t=PACK))
+            nc.vector.tensor_copy(gscale[:], tscale[:].indirect(idx[:]))
+
+        late = ctx.enter_context(tc.tile_pool(name="late", bufs=1))
         for q in range(4):
             r0 = SCALE_ROW0 + 4 * K_PASSES * q
-            nc.scalar.dma_start(
-                vs[32 * q : 32 * q + 4, :, :].bitcast(I32), gscale[r0 : r0 + 4 * K_PASSES, :].bitcast(I32)
-            )
-        load_table(2)
-        nc.sync.dma_start(w1last[:].bitcast(I32), w1_words[K_PASSES - 1].bitcast(I32))
-        nc.sync.dma_start(idx2[:], offs2)
-        ident = keep.tile([P, P], F32, name="ident")
-        make_identity(nc, ident[:])
+            queue = nc.sync if q % 2 == 0 else nc.scalar
+            queue.dma_start(vs[32 * q : 32 * q + 4, :, :].bitcast(I32), gscale[r0 : r0 + 4 * K_PASSES, :].bitcast(I32))
+        for a in range(1, K_PASSES):
+            load_table(late, a)
 
         compt = {}
-
-        def load_comp(h):
-            for g in range(H_PASSES):
-                compt[h, g] = keep.tile([P, PACK, HALF], F32, name="comp%d_%d" % (h, g))
-                nc.sync.dma_start(
-                    compt[h, g][:],
-                    comp[g * 512 : (g + 1) * 512, h * HALF : (h + 1) * HALF].rearrange("(c p) j -> p c j", p=P),
-                )
-
-        load_comp(0)
         w2raw = {}
-        wgot = keep.tile([P, S], F32, name="wgot")
-        for c in range(N // W2_COLS):
+        wgot = [late.tile([P, HALF], F32, name="wgo%d" % h) for h in range(2)]
+
+        def load_comp(first, width):
             for g in range(H_PASSES):
-                w2raw[c, g] = keep.tile([P, PACK, W2_COLS], F32, name="w2raw%d_%d" % (c, g))
+                t = late.tile([P, PACK, width], F32, name="comp%d_%d" % (first, g))
+                nc.sync.dma_start(
+                    t[:], comp[g * 512 : (g + 1) * 512, first : first + width].rearrange("(p t) j -> p t j", t=PACK)
+                )
+                for j in range(0, width, SUB):
+                    compt[(first + j) // SUB, g] = t[:, :, j : j + SUB]
+
+        def load_w2(c):
+            for g in range(H_PASSES):
+                w2raw[c, g] = late.tile([P, PACK, W2_COLS], F32, name="w2raw%d_%d" % (c, g))
                 nc.sync.dma_start(
                     w2raw[c, g][:],
                     w2[g * 512 : (g + 1) * 512, c * W2_COLS : (c + 1) * W2_COLS].rearrange("(p t) n -> p t n", t=PACK),
                 )
-            if c == 1:
-                nc.sync.dma_start(wgot[:], wgo)
-        load_comp(1)
+
+        load_comp(0, QUARTER)
+        load_w2(0)
+        nc.sync.dma_start(wgot[0][:], wgo[:, :HALF])
+        load_comp(QUARTER, QUARTER)
+        load_w2(1)
+        load_comp(HALF, HALF)
+        nc.sync.dma_start(wgot[1][:], wgo[:, HALF:])
 
         lncap = keep.tile([P, R_TILES], F32, name="lncap")
-        nlncap = keep.tile([P, R_TILES], F32, name="nlncap")
         rcap = keep.tile([P, R_TILES], F32, name="rcap")
-        capt = bank(7)
-        nc.tensor.transpose(capt[:, :P], caprows[:], ident[:])
-        nc.scalar.activation(lncap[:], capt[:, :R_TILES], ACT.Ln)
+        nc.scalar.activation(lncap[:], capt[:].rearrange("p g t -> p (g t)"), ACT.Ln)
         nc.scalar.activation(rcap[:], lncap[:], ACT.Exp, scale=-1.0)
-        nc.vector.tensor_scalar(nlncap[:], lncap[:], -1.0, None, ALU.mult)
+
+        w1c = keep.tile([P, K_PASSES * H], U16, name="w1c", align_bytes=64)
+        w1s = keep.tile([P, K_PASSES * H], U8, name="w1s", align_bytes=64)
+        for dst, src in ((w1c, w1raw), (w1s, w1sraw)):
+            nc.vector.tensor_copy(
+                dst[:].rearrange("p (b t m) -> p b t m", t=PACK, m=P),
+                src[:].rearrange("p a (g m t) -> p (a g) t m", t=PACK, m=P),
+            )
 
         vc = {}
         for a in range(K_PASSES - 1):
@@ -140,17 +147,18 @@ def tile_list_fraction_loading_kernel(
 
         xt = []
         for c in range(N_TILES // 2):
-            pair = ring.tile([P, 2, S], F32, name="x%d" % c, tag="big", bufs=K_PASSES)
+            pair = big_tile(ring if c == 0 else late, c, [P, 2, S], F32)
             nc.sync.dma_start(pair[:], x0[2 * c * P : (2 * c + 2) * P, :].rearrange("(c p) m -> p c m", p=P))
             xt.extend([pair[:, 0, :], pair[:, 1, :]])
 
         state = {}
 
         def mm1_pass(h, rt, a, acc):
+            cols = slice(a * H + rt * P, a * H + (rt + 1) * P)
             nc.tensor.matmul_mx(
                 out=acc[:],
-                lhsT=w1c[a][:, 2 * P * rt : 2 * P * (rt + 1)].bitcast(FP4X4),
-                lhsT_scale=w1s[:, a, P * rt : P * (rt + 1)],
+                lhsT=w1c[:, cols].bitcast(FP4X4),
+                lhsT_scale=w1s[:, cols],
                 rhs=vc[a, h].bitcast(FP8X4),
                 rhs_scale=vs[:, a, h * HALF : (h + 1) * HALF],
                 start=(a == 0),
@@ -161,53 +169,38 @@ def tile_list_fraction_loading_kernel(
             state["work", h] = ring.tile([P, SUBS_PER_HALF, R_TILES, SUB], F32, name="work%d" % h, tag="work", bufs=1)
 
         def expo(h, rt, acc):
-            nc.scalar.activation(
-                state["work", h][:, :, rt, :],
-                acc[:].rearrange("p (s j) -> p s j", j=SUB),
-                ACT.Exp,
-                bias=nlncap[:, rt : rt + 1],
-            )
+            nc.scalar.activation(state["work", h][:, :, rt, :], acc[:].rearrange("p (s j) -> p s j", j=SUB), ACT.Exp)
 
-        def prescale_vector(h, cols):
-            for rt in range(R_TILES):
-                t = compt[h, rt // PACK][:, rt % PACK, cols]
-                nc.vector.tensor_scalar(t, t, rcap[:, rt : rt + 1], None, ALU.mult)
-
-        def prescale_scalar(h, cols):
-            for rt in range(R_TILES):
-                t = compt[h, rt // PACK][:, rt % PACK, cols]
-                nc.scalar.activation(t, t, ACT.Copy, scale=rcap[:, rt : rt + 1])
-
-        def make_h(s, banks):
+        def add_comp(s):
             h, sl = divmod(s, SUBS_PER_HALF)
-            work = state["work", h]
-            cols = slice(sl * SUB, (sl + 1) * SUB)
-            dts = []
             for g in range(H_PASSES):
-                dt = bank(banks[g])
-                for c in range(PACK):
-                    o = dt[:, c * P : (c + 1) * P]
-                    nc.tensor.matmul(o, compt[h, g][:, c, cols], ident[:], start=True, stop=False, is_transpose=True)
-                    nc.tensor.matmul(o, work[:, sl, g * PACK + c, :], ident[:], start=False, stop=True, is_transpose=True)
-                dts.append(dt)
-            for g in range(H_PASSES):
-                nc.scalar.activation(
-                    work[:, sl, g * PACK : (g + 1) * PACK, :],
-                    dts[g][:].rearrange("j (p t) -> j t p", t=PACK),
-                    ACT.Abs_reciprocal_sqrt,
-                )
+                d = state["work", h][:, sl, g * PACK : (g + 1) * PACK, :]
+                nc.vector.tensor_tensor(d, d, compt[s, g], ALU.add)
 
-        def finish_h(s, banks):
+        def slot(s, g, width):
+            name = "slot%d_%d" % (s % SUBS_PER_HALF, g)
+            return ring.tile([P, width], F32, name=name, tag=name, bufs=1)
+
+        def root(s):
             h, sl = divmod(s, SUBS_PER_HALF)
-            work = state["work", h]
+            for g in range(H_PASSES):
+                u = slot(s, g, PACK * SUB)
+                for t in range(PACK):
+                    rt = g * PACK + t
+                    nc.scalar.activation(
+                        u[:, t * SUB : (t + 1) * SUB],
+                        state["work", h][:, sl, rt, :],
+                        ACT.Abs_reciprocal_sqrt,
+                        scale=rcap[:, rt : rt + 1],
+                    )
+                state["u", s, g] = u
+
+        def finish_h(s):
             hb = ring.tile([P, H_PASSES * SUB * PACK], BF16, name="hb", tag="hb", align_bytes=64)
             for g in range(H_PASSES):
-                bk = bank(banks[g])
-                for t in range(PACK):
-                    nc.tensor.transpose(bk[:, t * SUB : (t + 1) * SUB], work[:, sl, g * PACK + t, :], ident[:])
                 nc.scalar.activation(
-                    hb[:, g * BANK : (g + 1) * BANK].rearrange("p (j t) -> p j t", t=PACK),
-                    bk[:].rearrange("p (t j) -> p j t", t=PACK),
+                    hb[:, g * BANK : (g + 1) * BANK].rearrange("p (c i t) -> p c t i", i=4, t=PACK),
+                    state["u", s, g][:].rearrange("p (t c i) -> p c t i", i=4, t=PACK),
                     ACT.Square,
                 )
             hc = ring.tile([P, H_PASSES * SUB], U32, name="hc", tag="hc", bufs=4, align_bytes=64)
@@ -218,7 +211,7 @@ def tile_list_fraction_loading_kernel(
         w2c, w2s = [], []
 
         def quantize_w2(c):
-            w2b = ring.tile([P, H_PASSES * W2_COLS * PACK], BF16, name="w2b", tag="w2b", align_bytes=64)
+            w2b = ring.tile([P, H_PASSES * W2_COLS * PACK], BF16, name="w2b", tag="w2b", bufs=1, align_bytes=64)
             for g in range(H_PASSES):
                 nc.vector.tensor_copy(
                     w2b[:, g * W2_COLS * PACK : (g + 1) * W2_COLS * PACK].rearrange("p (c i t) -> p c t i", i=4, t=PACK),
@@ -226,7 +219,10 @@ def tile_list_fraction_loading_kernel(
                 )
             codes = keep.tile([P, H_PASSES * W2_COLS], U32, name="w2c%d" % c, align_bytes=64)
             scales = keep.tile([P, H_PASSES * W2_COLS], U8, name="w2s%d" % c, align_bytes=64)
-            nc.vector.quantize_mx(out=codes[:].bitcast(FP8X4), scales=scales[:], in_=w2b[:])
+            for lo, hi in ((0, 256), (256, 768)):
+                nc.vector.quantize_mx(
+                    out=codes[:, lo:hi].bitcast(FP8X4), scales=scales[:, lo:hi], in_=w2b[:, PACK * lo : PACK * hi]
+                )
             w2c.append(codes)
             w2s.append(scales)
 
@@ -235,38 +231,42 @@ def tile_list_fraction_loading_kernel(
         def finish_out(nt, pieces=1):
             for i in range(pieces):
                 m = slice(i * S // pieces, (i + 1) * S // pieces)
-                nc.vector.scalar_tensor_tensor(xt[nt][:, m], pages[nt][:, m], 1.0, xt[nt][:, m], ALU.add, ALU.mult)
+                gain = ring.tile([P, S // pieces], F32, name="gain", tag="gain")
+                nc.scalar.activation(gain[:], pages[nt][:, m], ACT.Identity, bias=1.0)
+                nc.vector.tensor_tensor(xt[nt][:, m], gain[:], xt[nt][:, m], ALU.mult)
                 nc.sync.dma_start(out[nt * P : (nt + 1) * P, m], xt[nt][:, m])
 
-        def place(s, part, b):
+        def place(s, part, b, behind=None):
             hc, hs = state["hq", s]
             acc = bank(b)
             for i in range(Y_TILES):
-                nt = part * Y_TILES + i
-                c, off = divmod(nt * P, W2_COLS)
                 for g in range(H_PASSES):
-                    w = slice(g * W2_COLS + off, g * W2_COLS + off + P)
+                    w = slice(g * W2_COLS + i * P, g * W2_COLS + (i + 1) * P)
                     nc.tensor.matmul_mx(
                         out=acc[:, i * SUB : (i + 1) * SUB],
-                        lhsT=w2c[c][:, w].bitcast(FP8X4),
-                        lhsT_scale=w2s[c][:, w],
+                        lhsT=w2c[part][:, w].bitcast(FP8X4),
+                        lhsT_scale=w2s[part][:, w],
                         rhs=hc[:, g * SUB : (g + 1) * SUB].bitcast(FP8X4),
                         rhs_scale=hs[:, g * SUB : (g + 1) * SUB],
                         start=(g == 0),
                         stop=(g == H_PASSES - 1),
                     )
-            y = ring.tile([P, Y_TILES * SUB], F32, name="y", tag="y", bufs=8)
+            if behind is None:
+                y = ring.tile([P, Y_TILES * SUB], F32, name="y", tag="y", bufs=4)
+            else:
+                y = slot(behind[0], behind[1], Y_TILES * SUB)
             nc.scalar.copy(y[:], acc[:, : Y_TILES * SUB])
+            h, sl = divmod(s, SUBS_PER_HALF)
             for i in range(Y_TILES):
                 nt = part * Y_TILES + i
                 nc.vector.tensor_tensor(
                     pages[nt][:].indirect(idx2[:, s * SUB // 16 : (s + 1) * SUB // 16]),
                     y[:, i * SUB : (i + 1) * SUB],
-                    wgot[:, s * SUB : (s + 1) * SUB],
+                    wgot[h][:, sl * SUB : (sl + 1) * SUB],
                     ALU.mult,
                 )
-                if s == S // SUB - 1 and nt > 0:
-                    finish_out(nt - 1)
+                if s == S // SUB - 1 and nt > 1:
+                    finish_out(nt - 2)
 
         accs = [bank(rt) for rt in range(R_TILES)]
         for a in range(K_PASSES):
@@ -275,50 +275,54 @@ def tile_list_fraction_loading_kernel(
         new_work(0)
         for rt in range(R_TILES):
             expo(0, rt, accs[rt])
-        prescale_vector(0, slice(0, HALF))
         quantize_w2(0)
+        add_comp(0)
+        root(0)
+        finish_h(0)
+        add_comp(1)
+        root(1)
+        place(0, 0, 5)
+        finish_h(1)
+        add_comp(2)
+        add_comp(3)
         quantize_w2(1)
-        make_h(0, (0, 1))
-        finish_h(0, (4, 5))
-        quantize_w2(2)
-        make_h(1, (2, 3))
-        place(0, 0, 6)
-        finish_h(1, (7, 4))
-        place(0, 1, 7)
-        make_h(2, (0, 1))
-        finish_h(2, (5, 6))
-        place(1, 0, 5)
-        make_h(3, (2, 3))
-        finish_h(3, (4, 7))
-        place(1, 1, 4)
-        place(2, 0, 7)
+        root(2)
+        finish_h(2)
+        place(1, 0, 6, (2, 0))
+        root(3)
+        finish_h(3)
+        place(0, 1, 7, (3, 0))
+        place(1, 1, 5, (3, 1))
         new_work(1)
-        prescale_vector(1, slice(0, 2 * SUB))
-        for rt, b in enumerate((0, 1, 2, 3, 6, 5, 0, 1)):
+        for rt, b in enumerate((0, 1, 2, 3, 4, 0, 2, 3)):
             acc = bank(b)
             for a in range(K_PASSES):
                 mm1_pass(1, rt, a, acc)
             expo(1, rt, acc)
-            if rt == 2:
-                place(2, 1, 2)
-            if rt == 5:
-                place(3, 0, 6)
-        make_h(4, (4, 7))
-        finish_h(4, (0, 1))
-        place(3, 1, 0)
-        make_h(5, (3, 2))
-        place(4, 0, 5)
-        finish_h(5, (6, 1))
-        place(4, 1, 6)
-        prescale_scalar(1, slice(2 * SUB, HALF))
-        make_h(6, (4, 7))
-        finish_h(6, (0, 5))
-        place(5, 0, 0)
-        make_h(7, (3, 2))
-        finish_h(7, (1, 6))
-        place(5, 1, 1)
-        place(6, 0, 6)
-        place(6, 1, 3)
-        place(7, 0, 4)
-        place(7, 1, 7)
+            if rt == 1:
+                place(2, 0, 1)
+        add_comp(4)
+        add_comp(5)
+        place(2, 1, 3)
+        root(4)
+        finish_h(4)
+        add_comp(6)
+        add_comp(7)
+        place(3, 0, 6, (4, 0))
+        root(5)
+        finish_h(5)
+        place(3, 1, 7, (5, 0))
+        place(4, 0, 5, (5, 1))
+        root(6)
+        finish_h(6)
+        place(4, 1, 0, (6, 0))
+        place(5, 0, 1, (6, 1))
+        root(7)
+        finish_h(7)
+        place(5, 1, 2, (7, 0))
+        place(6, 0, 3, (7, 1))
+        place(6, 1, 4)
+        place(7, 0, 5)
+        place(7, 1, 6)
+        finish_out(N_TILES - 2)
         finish_out(N_TILES - 1, 2)

@@ -1,6 +1,7 @@
 from contextlib import ExitStack
 
 import concourse.mybir as mybir
+from concourse.masks import make_identity
 
 K, H, N, T, S = 1536, 1024, 768, 4096, 1024
 FLOPS = 2 * K * H * S + 2 * H * N * S
@@ -18,18 +19,27 @@ ALU = mybir.AluOpType
 
 P = 128
 PACK = 4
+PASS = P * PACK
 BANK = 512
-K_PASSES = K // (P * PACK)
-H_PASSES = H // (P * PACK)
+K_PASSES = K // PASS
+R_PASSES = H // PASS
 R_TILES = H // P
 N_TILES = N // P
 HALF = 512
-SUB = 128
 QUARTER = 256
-SUBS_PER_HALF = HALF // SUB
-Y_TILES = 3
-W2_COLS = Y_TILES * P
-SCALE_ROW0 = 16
+PIECE = 128
+PIECES = S // PIECE
+PIECES_PER_HALF = HALF // PIECE
+PART_TILES = 3
+PART_COLS = PART_TILES * P
+LIST_ROWS = 16
+SCALE_ROWS = 16
+QUADRANT = 32
+QUADRANT_ROWS = 4
+STAGED_ROW0 = 16
+STAGED_ROWS = SCALE_ROWS * K_PASSES
+LINE = 4
+W2_WORD_RUNS = ((0, 256), (256, 768))
 
 
 def tile_list_fraction_loading_kernel(
@@ -41,288 +51,323 @@ def tile_list_fraction_loading_kernel(
         ring = ctx.enter_context(tc.tile_pool(name="ring", bufs=2))
         psum = ctx.enter_context(tc.psum_pool(name="psum", bufs=1))
 
-        def bank(b):
-            return psum.tile([P, BANK], F32, name="bank%d" % b, tag="bank%d" % b)
+        def bank(number):
+            return psum.tile([P, BANK], F32, name="bank%d" % number, tag="bank%d" % number)
 
-        idx = keep.tile([P, S // 16], U16, name="idx")
-        idx2 = keep.tile([P, S // 16], U16, name="idx2")
-        w1raw = ring.tile([P, K_PASSES, H], U16, name="w1raw", tag="work", bufs=1)
-        w1sraw = ring.tile([P, K_PASSES, H], U8, name="w1sraw", tag="w2b", bufs=1, align_bytes=64)
-        capt = keep.tile([P, H_PASSES, PACK], F32, name="capt")
-        vs = keep.tile([P, K_PASSES, S], U8, name="vs", align_bytes=64)
-        gscale = keep.tile([P, S], U8, name="gscale")
+        def big_tile(pool, number, shape, dtype):
+            return pool.tile(shape, dtype, name="big%d" % number, tag="big%d" % number, bufs=1)
+
+        idx = keep.tile([P, S // LIST_ROWS], U16, name="idx")
+        idx2 = keep.tile([P, S // LIST_ROWS], U16, name="idx2")
+        w1_words_in = ring.tile([P, K_PASSES, H], U16, name="w1_words_in", tag="work", bufs=1)
+        w1_scales_in = ring.tile([P, K_PASSES, H], U8, name="w1_scales_in", tag="w2_bf16", bufs=1, align_bytes=64)
+        cap_sb = keep.tile([P, R_PASSES, PACK], F32, name="cap_sb")
+        v_scales = keep.tile([P, K_PASSES, S], U8, name="v_scales", align_bytes=64)
+        picked_scales = keep.tile([P, S], U8, name="picked_scales")
         table = []
-
-        def big_tile(pool, i, shape, dtype):
-            return pool.tile(shape, dtype, name="big%d" % i, tag="big%d" % i, bufs=1)
 
         def load_table(pool, a):
             table.append(big_tile(pool, a, [P, T], U32))
-            nc.sync.dma_start(table[a][:].bitcast(I32), tab_words[a].rearrange("p t i -> p (t i)").bitcast(I32))
+            nc.sync.dma_start(table[a][:].bitcast(I32), tab_words[a].rearrange("p c i -> p (c i)").bitcast(I32))
 
         with tc.tile_pool(name="early", bufs=1) as early:
-            tscale = early.tile([P, T], U8, name="tscale")
-            nc.vector.memset(w1sraw[:].bitcast(I32), 0)
-            nc.vector.memset(tscale[0:SCALE_ROW0, :].bitcast(I32), 0)
-            nc.vector.memset(tscale[64:P, :].bitcast(I32), 0)
-            nc.vector.memset(vs[:].bitcast(I32), 0)
+            staged_scales = early.tile([P, T], U8, name="staged_scales")
+            nc.vector.memset(w1_scales_in[:].bitcast(I32), 0)
+            nc.vector.memset(staged_scales[0:STAGED_ROW0, :].bitcast(I32), 0)
+            nc.vector.memset(staged_scales[STAGED_ROW0 + STAGED_ROWS : P, :].bitcast(I32), 0)
+            nc.vector.memset(v_scales[:].bitcast(I32), 0)
 
             nc.sync.dma_start(idx[:], offs)
             nc.sync.dma_start(
-                tscale[SCALE_ROW0 : SCALE_ROW0 + 16 * K_PASSES, :].bitcast(I32),
-                tab_scales.rearrange("a q t -> q a t").bitcast(I32),
+                staged_scales[STAGED_ROW0 : STAGED_ROW0 + STAGED_ROWS, :].bitcast(I32),
+                tab_scales.rearrange("a q c -> q a c").bitcast(I32),
             )
             nc.sync.dma_start(idx2[:], offs2)
-            nc.sync.dma_start(w1raw[:].bitcast(I32), w1_words.rearrange("a p n -> p a n").bitcast(I32))
-            for q in range(4):
+            nc.sync.dma_start(w1_words_in[:].bitcast(I32), w1_words.rearrange("a p c -> p a c").bitcast(I32))
+            for quad in range(P // QUADRANT):
+                rows = slice(QUADRANT_ROWS * quad, QUADRANT_ROWS * (quad + 1))
                 nc.sync.dma_start(
-                    w1sraw[32 * q : 32 * q + 4, :, :].bitcast(I32),
-                    w1_scales[:, 4 * q : 4 * q + 4, :].rearrange("a r n -> r a n").bitcast(I32),
+                    w1_scales_in[QUADRANT * quad : QUADRANT * quad + QUADRANT_ROWS, :, :].bitcast(I32),
+                    w1_scales[:, rows, :].rearrange("a q c -> q a c").bitcast(I32),
                 )
             load_table(ring, 0)
-            nc.gpsimd.dma_start(capt[:], cap.rearrange("(g p t) -> p g t", p=P, t=PACK))
-            nc.vector.tensor_copy(gscale[:], tscale[:].indirect(idx[:]))
+            nc.gpsimd.dma_start(cap_sb[:], cap.rearrange("(g p t) -> p g t", p=P, t=PACK))
+            nc.vector.tensor_copy(picked_scales[:], staged_scales[:].indirect(idx[:]))
 
         late = ctx.enter_context(tc.tile_pool(name="late", bufs=1))
-        for q in range(4):
-            r0 = SCALE_ROW0 + 4 * K_PASSES * q
-            queue = nc.sync if q % 2 == 0 else nc.scalar
-            queue.dma_start(vs[32 * q : 32 * q + 4, :, :].bitcast(I32), gscale[r0 : r0 + 4 * K_PASSES, :].bitcast(I32))
+        for quad in range(P // QUADRANT):
+            row0 = STAGED_ROW0 + QUADRANT_ROWS * K_PASSES * quad
+            queue = nc.sync if quad % 2 == 0 else nc.scalar
+            queue.dma_start(
+                v_scales[QUADRANT * quad : QUADRANT * quad + QUADRANT_ROWS, :, :].bitcast(I32),
+                picked_scales[row0 : row0 + QUADRANT_ROWS * K_PASSES, :].bitcast(I32),
+            )
         for a in range(1, K_PASSES):
             load_table(late, a)
 
-        compt = {}
-        w2raw = {}
-        wgot = [late.tile([P, HALF], F32, name="wgo%d" % h) for h in range(2)]
+        comp_sb = {}
+        w2_in = {}
+        wgo_sb = [late.tile([P, HALF], F32, name="wgo%d" % half) for half in range(S // HALF)]
 
         def load_comp(first, width):
-            for g in range(H_PASSES):
-                t = late.tile([P, PACK, width], F32, name="comp%d_%d" % (first, g))
+            for g in range(R_PASSES):
+                rows = late.tile([P, PACK, width], F32, name="comp%d_%d" % (first, g))
                 nc.sync.dma_start(
-                    t[:], comp[g * 512 : (g + 1) * 512, first : first + width].rearrange("(p t) j -> p t j", t=PACK)
+                    rows[:],
+                    comp[g * PASS : (g + 1) * PASS, first : first + width].rearrange("(p t) j -> p t j", t=PACK),
                 )
-                for j in range(0, width, SUB):
-                    compt[(first + j) // SUB, g] = t[:, :, j : j + SUB]
+                for j in range(0, width, PIECE):
+                    comp_sb[(first + j) // PIECE, g] = rows[:, :, j : j + PIECE]
 
-        def load_w2(c):
-            for g in range(H_PASSES):
-                w2raw[c, g] = late.tile([P, PACK, W2_COLS], F32, name="w2raw%d_%d" % (c, g))
+        def load_w2(part):
+            cols = slice(part * PART_COLS, (part + 1) * PART_COLS)
+            for g in range(R_PASSES):
+                w2_in[part, g] = late.tile([P, PACK, PART_COLS], F32, name="w2_in%d_%d" % (part, g))
                 nc.sync.dma_start(
-                    w2raw[c, g][:],
-                    w2[g * 512 : (g + 1) * 512, c * W2_COLS : (c + 1) * W2_COLS].rearrange("(p t) n -> p t n", t=PACK),
+                    w2_in[part, g][:], w2[g * PASS : (g + 1) * PASS, cols].rearrange("(p t) n -> p t n", t=PACK)
                 )
 
         load_comp(0, QUARTER)
         load_w2(0)
-        nc.sync.dma_start(wgot[0][:], wgo[:, :HALF])
+        nc.sync.dma_start(wgo_sb[0][:], wgo[:, :HALF])
         load_comp(QUARTER, QUARTER)
         load_w2(1)
         load_comp(HALF, HALF)
-        nc.sync.dma_start(wgot[1][:], wgo[:, HALF:])
+        nc.sync.dma_start(wgo_sb[1][:], wgo[:, HALF:])
 
-        lncap = keep.tile([P, R_TILES], F32, name="lncap")
-        rcap = keep.tile([P, R_TILES], F32, name="rcap")
-        nc.scalar.activation(lncap[:], capt[:].rearrange("p g t -> p (g t)"), ACT.Ln)
-        nc.scalar.activation(rcap[:], lncap[:], ACT.Exp, scale=-1.0)
+        log_cap = keep.tile([P, R_TILES], F32, name="log_cap")
+        inv_cap = keep.tile([P, R_TILES], F32, name="inv_cap")
+        nc.scalar.activation(log_cap[:], cap_sb[:].rearrange("p g t -> p (g t)"), ACT.Ln)
+        nc.scalar.activation(inv_cap[:], log_cap[:], ACT.Exp, scale=-1.0)
+        ident = keep.tile([P, P], F32, name="ident")
+        make_identity(nc, ident[:])
 
-        w1c = keep.tile([P, K_PASSES * H], U16, name="w1c", align_bytes=64)
-        w1s = keep.tile([P, K_PASSES * H], U8, name="w1s", align_bytes=64)
-        for dst, src in ((w1c, w1raw), (w1s, w1sraw)):
+        w1_codes = keep.tile([P, K_PASSES * H], U16, name="w1_codes", align_bytes=64)
+        w1_planes = keep.tile([P, K_PASSES * H], U8, name="w1_planes", align_bytes=64)
+        for ordered, arrived in ((w1_codes, w1_words_in), (w1_planes, w1_scales_in)):
             nc.vector.tensor_copy(
-                dst[:].rearrange("p (b t m) -> p b t m", t=PACK, m=P),
-                src[:].rearrange("p a (g m t) -> p (a g) t m", t=PACK, m=P),
+                ordered[:].rearrange("p (b t m) -> p b t m", t=PACK, m=P),
+                arrived[:].rearrange("p a (g m t) -> p (a g) t m", t=PACK, m=P),
             )
 
-        vc = {}
+        v_codes = {}
         for a in range(K_PASSES - 1):
-            whole = keep.tile([P, S], U32, name="vc%d" % a, align_bytes=64)
+            whole = keep.tile([P, S], U32, name="v_codes%d" % a, align_bytes=64)
             nc.vector.tensor_copy(whole[:], table[a][:].indirect(idx[:]))
-            for h in range(2):
-                vc[a, h] = whole[:, h * HALF : (h + 1) * HALF]
-        a = K_PASSES - 1
-        for h in range(2):
-            part = keep.tile([P, HALF], U32, name="vc%d_%d" % (a, h), align_bytes=64)
-            nc.vector.tensor_copy(part[:], table[a][:].indirect(idx[:, h * HALF // 16 : (h + 1) * HALF // 16]))
-            vc[a, h] = part[:]
+            for half in range(S // HALF):
+                v_codes[a, half] = whole[:, half * HALF : (half + 1) * HALF]
+        last = K_PASSES - 1
+        for half in range(S // HALF):
+            picked = keep.tile([P, HALF], U32, name="v_codes%d_%d" % (last, half), align_bytes=64)
+            entries = idx[:, half * HALF // LIST_ROWS : (half + 1) * HALF // LIST_ROWS]
+            nc.vector.tensor_copy(picked[:], table[last][:].indirect(entries))
+            v_codes[last, half] = picked[:]
 
-        xt = []
-        for c in range(N_TILES // 2):
-            pair = big_tile(ring if c == 0 else late, c, [P, 2, S], F32)
-            nc.sync.dma_start(pair[:], x0[2 * c * P : (2 * c + 2) * P, :].rearrange("(c p) m -> p c m", p=P))
-            xt.extend([pair[:, 0, :], pair[:, 1, :]])
+        x_sb = []
+        for pair in range(N_TILES // 2):
+            both = big_tile(ring if pair == 0 else late, pair, [P, 2, S], F32)
+            nc.sync.dma_start(both[:], x0[2 * pair * P : (2 * pair + 2) * P, :].rearrange("(c p) m -> p c m", p=P))
+            x_sb.extend([both[:, 0, :], both[:, 1, :]])
 
-        state = {}
+        work = []
+        denominators = {}
+        roots = {}
+        h_mx = {}
+        w2_mx = []
+        pages = [keep.tile([P, S], F32, name="page%d" % nt) for nt in range(N_TILES)]
 
-        def mm1_pass(h, rt, a, acc):
+        def first_product(half, rt, a, acc):
             cols = slice(a * H + rt * P, a * H + (rt + 1) * P)
             nc.tensor.matmul_mx(
                 out=acc[:],
-                lhsT=w1c[:, cols].bitcast(FP4X4),
-                lhsT_scale=w1s[:, cols],
-                rhs=vc[a, h].bitcast(FP8X4),
-                rhs_scale=vs[:, a, h * HALF : (h + 1) * HALF],
+                lhsT=w1_codes[:, cols].bitcast(FP4X4),
+                lhsT_scale=w1_planes[:, cols],
+                rhs=v_codes[a, half].bitcast(FP8X4),
+                rhs_scale=v_scales[:, a, half * HALF : (half + 1) * HALF],
                 start=(a == 0),
                 stop=(a == K_PASSES - 1),
             )
 
-        def new_work(h):
-            state["work", h] = ring.tile([P, SUBS_PER_HALF, R_TILES, SUB], F32, name="work%d" % h, tag="work", bufs=1)
+        def open_half():
+            work.append(ring.tile([P, PIECES_PER_HALF, R_TILES, PIECE], F32, name="work", tag="work", bufs=1))
 
-        def expo(h, rt, acc):
-            nc.scalar.activation(state["work", h][:, :, rt, :], acc[:].rearrange("p (s j) -> p s j", j=SUB), ACT.Exp)
+        def exponential(half, rt, acc):
+            nc.scalar.activation(work[half][:, :, rt, :], acc[:].rearrange("p (s j) -> p s j", j=PIECE), ACT.Exp)
 
-        def add_comp(s):
-            h, sl = divmod(s, SUBS_PER_HALF)
-            for g in range(H_PASSES):
-                d = state["work", h][:, sl, g * PACK : (g + 1) * PACK, :]
-                nc.vector.tensor_tensor(d, d, compt[s, g], ALU.add)
+        def exponentials_of(piece, g):
+            half, within = divmod(piece, PIECES_PER_HALF)
+            return work[half][:, within, g * PACK : (g + 1) * PACK, :]
 
-        def slot(s, g, width):
-            name = "slot%d_%d" % (s % SUBS_PER_HALF, g)
+        def add_comp(piece):
+            for g in range(R_PASSES):
+                values = exponentials_of(piece, g)
+                nc.vector.tensor_tensor(values, values, comp_sb[piece, g], ALU.add)
+                denominators[piece, g] = values
+
+        def add_comp_by_transposes(piece, there, back):
+            for g in range(R_PASSES):
+                values = exponentials_of(piece, g)
+                acc = bank(there[g])
+                for t in range(PACK):
+                    turned = acc[:, t * P : (t + 1) * P]
+                    nc.tensor.matmul(
+                        turned, comp_sb[piece, g][:, t, :], ident[:], start=True, stop=False, is_transpose=True
+                    )
+                    nc.tensor.matmul(turned, values[:, t, :], ident[:], start=False, stop=True, is_transpose=True)
+                nc.scalar.copy(values, acc[:].rearrange("j (t p) -> j t p", t=PACK))
+            for g in range(R_PASSES):
+                values = exponentials_of(piece, g)
+                acc = bank(back[g])
+                for t in range(PACK):
+                    nc.tensor.transpose(acc[:, t * PIECE : (t + 1) * PIECE], values[:, t, :], ident[:])
+                denominators[piece, g] = acc[:].rearrange("p (t j) -> p t j", t=PACK)
+
+        def root_buffer(piece, g, width):
+            name = "root%d_%d" % (piece % PIECES_PER_HALF, g)
             return ring.tile([P, width], F32, name=name, tag=name, bufs=1)
 
-        def root(s):
-            h, sl = divmod(s, SUBS_PER_HALF)
-            for g in range(H_PASSES):
-                u = slot(s, g, PACK * SUB)
+        def make_h(piece):
+            for g in range(R_PASSES):
+                roots[piece, g] = root_buffer(piece, g, PACK * PIECE)
                 for t in range(PACK):
                     rt = g * PACK + t
                     nc.scalar.activation(
-                        u[:, t * SUB : (t + 1) * SUB],
-                        state["work", h][:, sl, rt, :],
+                        roots[piece, g][:, t * PIECE : (t + 1) * PIECE],
+                        denominators[piece, g][:, t, :],
                         ACT.Abs_reciprocal_sqrt,
-                        scale=rcap[:, rt : rt + 1],
+                        scale=inv_cap[:, rt : rt + 1],
                     )
-                state["u", s, g] = u
 
-        def finish_h(s):
-            hb = ring.tile([P, H_PASSES * SUB * PACK], BF16, name="hb", tag="hb", align_bytes=64)
-            for g in range(H_PASSES):
+        def quantize_h(piece):
+            h_bf16 = ring.tile([P, R_PASSES * PIECE * PACK], BF16, name="h_bf16", tag="h_bf16", align_bytes=64)
+            for g in range(R_PASSES):
                 nc.scalar.activation(
-                    hb[:, g * BANK : (g + 1) * BANK].rearrange("p (c i t) -> p c t i", i=4, t=PACK),
-                    state["u", s, g][:].rearrange("p (t c i) -> p c t i", i=4, t=PACK),
+                    h_bf16[:, g * PIECE * PACK : (g + 1) * PIECE * PACK].rearrange(
+                        "p (c i t) -> p c t i", i=LINE, t=PACK
+                    ),
+                    roots[piece, g][:].rearrange("p (t c i) -> p c t i", i=LINE, t=PACK),
                     ACT.Square,
                 )
-            hc = ring.tile([P, H_PASSES * SUB], U32, name="hc", tag="hc", bufs=4, align_bytes=64)
-            hs = ring.tile([P, H_PASSES * SUB], U8, name="hs", tag="hs", bufs=4, align_bytes=64)
-            nc.vector.quantize_mx(out=hc[:].bitcast(FP8X4), scales=hs[:], in_=hb[:])
-            state["hq", s] = (hc, hs)
+            codes = ring.tile([P, R_PASSES * PIECE], U32, name="h_codes", tag="h_codes", bufs=4, align_bytes=64)
+            scales = ring.tile([P, R_PASSES * PIECE], U8, name="h_scales", tag="h_scales", bufs=4, align_bytes=64)
+            nc.vector.quantize_mx(out=codes[:].bitcast(FP8X4), scales=scales[:], in_=h_bf16[:])
+            h_mx[piece] = (codes, scales)
 
-        w2c, w2s = [], []
-
-        def quantize_w2(c):
-            w2b = ring.tile([P, H_PASSES * W2_COLS * PACK], BF16, name="w2b", tag="w2b", bufs=1, align_bytes=64)
-            for g in range(H_PASSES):
+        def quantize_w2(part):
+            width = PART_COLS * PACK
+            w2_bf16 = ring.tile([P, R_PASSES * width], BF16, name="w2_bf16", tag="w2_bf16", bufs=1, align_bytes=64)
+            for g in range(R_PASSES):
                 nc.vector.tensor_copy(
-                    w2b[:, g * W2_COLS * PACK : (g + 1) * W2_COLS * PACK].rearrange("p (c i t) -> p c t i", i=4, t=PACK),
-                    w2raw[c, g][:].rearrange("p t (c i) -> p c t i", i=4),
+                    w2_bf16[:, g * width : (g + 1) * width].rearrange("p (c i t) -> p c t i", i=LINE, t=PACK),
+                    w2_in[part, g][:].rearrange("p t (c i) -> p c t i", i=LINE),
                 )
-            codes = keep.tile([P, H_PASSES * W2_COLS], U32, name="w2c%d" % c, align_bytes=64)
-            scales = keep.tile([P, H_PASSES * W2_COLS], U8, name="w2s%d" % c, align_bytes=64)
-            for lo, hi in ((0, 256), (256, 768)):
+            codes = keep.tile([P, R_PASSES * PART_COLS], U32, name="w2_codes%d" % part, align_bytes=64)
+            scales = keep.tile([P, R_PASSES * PART_COLS], U8, name="w2_scales%d" % part, align_bytes=64)
+            for lo, hi in W2_WORD_RUNS:
                 nc.vector.quantize_mx(
-                    out=codes[:, lo:hi].bitcast(FP8X4), scales=scales[:, lo:hi], in_=w2b[:, PACK * lo : PACK * hi]
+                    out=codes[:, lo:hi].bitcast(FP8X4), scales=scales[:, lo:hi], in_=w2_bf16[:, PACK * lo : PACK * hi]
                 )
-            w2c.append(codes)
-            w2s.append(scales)
+            w2_mx.append((codes, scales))
 
-        pages = [keep.tile([P, S], F32, name="page%d" % nt) for nt in range(N_TILES)]
+        def finish(nt, stores=1):
+            for i in range(stores):
+                cols = slice(i * S // stores, (i + 1) * S // stores)
+                gain = ring.tile([P, S // stores], F32, name="gain", tag="gain")
+                nc.scalar.activation(gain[:], pages[nt][:, cols], ACT.Identity, bias=1.0)
+                nc.vector.tensor_tensor(x_sb[nt][:, cols], gain[:], x_sb[nt][:, cols], ALU.mult)
+                nc.sync.dma_start(out[nt * P : (nt + 1) * P, cols], x_sb[nt][:, cols])
 
-        def finish_out(nt, pieces=1):
-            for i in range(pieces):
-                m = slice(i * S // pieces, (i + 1) * S // pieces)
-                gain = ring.tile([P, S // pieces], F32, name="gain", tag="gain")
-                nc.scalar.activation(gain[:], pages[nt][:, m], ACT.Identity, bias=1.0)
-                nc.vector.tensor_tensor(xt[nt][:, m], gain[:], xt[nt][:, m], ALU.mult)
-                nc.sync.dma_start(out[nt * P : (nt + 1) * P, m], xt[nt][:, m])
-
-        def place(s, part, b, behind=None):
-            hc, hs = state["hq", s]
-            acc = bank(b)
-            for i in range(Y_TILES):
-                for g in range(H_PASSES):
-                    w = slice(g * W2_COLS + i * P, g * W2_COLS + (i + 1) * P)
+        def place(piece, part, number, behind=None):
+            h_codes, h_scales = h_mx[piece]
+            w2_codes, w2_scales = w2_mx[part]
+            acc = bank(number)
+            for i in range(PART_TILES):
+                for g in range(R_PASSES):
+                    cols = slice(g * PART_COLS + i * P, g * PART_COLS + (i + 1) * P)
                     nc.tensor.matmul_mx(
-                        out=acc[:, i * SUB : (i + 1) * SUB],
-                        lhsT=w2c[part][:, w].bitcast(FP8X4),
-                        lhsT_scale=w2s[part][:, w],
-                        rhs=hc[:, g * SUB : (g + 1) * SUB].bitcast(FP8X4),
-                        rhs_scale=hs[:, g * SUB : (g + 1) * SUB],
+                        out=acc[:, i * PIECE : (i + 1) * PIECE],
+                        lhsT=w2_codes[:, cols].bitcast(FP8X4),
+                        lhsT_scale=w2_scales[:, cols],
+                        rhs=h_codes[:, g * PIECE : (g + 1) * PIECE].bitcast(FP8X4),
+                        rhs_scale=h_scales[:, g * PIECE : (g + 1) * PIECE],
                         start=(g == 0),
-                        stop=(g == H_PASSES - 1),
+                        stop=(g == R_PASSES - 1),
                     )
             if behind is None:
-                y = ring.tile([P, Y_TILES * SUB], F32, name="y", tag="y", bufs=4)
+                y = ring.tile([P, PART_TILES * PIECE], F32, name="y", tag="y", bufs=4)
             else:
-                y = slot(behind[0], behind[1], Y_TILES * SUB)
-            nc.scalar.copy(y[:], acc[:, : Y_TILES * SUB])
-            h, sl = divmod(s, SUBS_PER_HALF)
-            for i in range(Y_TILES):
-                nt = part * Y_TILES + i
+                y = root_buffer(behind[0], behind[1], PART_TILES * PIECE)
+            nc.scalar.copy(y[:], acc[:, : PART_TILES * PIECE])
+            half, within = divmod(piece, PIECES_PER_HALF)
+            places = idx2[:, piece * PIECE // LIST_ROWS : (piece + 1) * PIECE // LIST_ROWS]
+            for i in range(PART_TILES):
+                nt = part * PART_TILES + i
                 nc.vector.tensor_tensor(
-                    pages[nt][:].indirect(idx2[:, s * SUB // 16 : (s + 1) * SUB // 16]),
-                    y[:, i * SUB : (i + 1) * SUB],
-                    wgot[h][:, sl * SUB : (sl + 1) * SUB],
+                    pages[nt][:].indirect(places),
+                    y[:, i * PIECE : (i + 1) * PIECE],
+                    wgo_sb[half][:, within * PIECE : (within + 1) * PIECE],
                     ALU.mult,
                 )
-                if s == S // SUB - 1 and nt > 1:
-                    finish_out(nt - 2)
+                if piece == PIECES - 1 and nt >= 2:
+                    finish(nt - 2)
+
 
         accs = [bank(rt) for rt in range(R_TILES)]
         for a in range(K_PASSES):
             for rt in range(R_TILES):
-                mm1_pass(0, rt, a, accs[rt])
-        new_work(0)
+                first_product(0, rt, a, accs[rt])
+        open_half()
         for rt in range(R_TILES):
-            expo(0, rt, accs[rt])
+            exponential(0, rt, accs[rt])
         quantize_w2(0)
         add_comp(0)
-        root(0)
-        finish_h(0)
+        make_h(0)
+        quantize_h(0)
         add_comp(1)
-        root(1)
+        make_h(1)
         place(0, 0, 5)
-        finish_h(1)
+        quantize_h(1)
         add_comp(2)
         add_comp(3)
         quantize_w2(1)
-        root(2)
-        finish_h(2)
-        place(1, 0, 6, (2, 0))
-        root(3)
-        finish_h(3)
-        place(0, 1, 7, (3, 0))
-        place(1, 1, 5, (3, 1))
-        new_work(1)
-        for rt, b in enumerate((0, 1, 2, 3, 4, 0, 2, 3)):
-            acc = bank(b)
+        make_h(2)
+        quantize_h(2)
+        place(1, 0, 6, behind=(2, 0))
+        make_h(3)
+        quantize_h(3)
+        place(0, 1, 7, behind=(3, 0))
+        place(1, 1, 5, behind=(3, 1))
+
+        open_half()
+        for rt, number in enumerate((0, 1, 2, 3, 4, 0, 2, 3)):
+            acc = bank(number)
             for a in range(K_PASSES):
-                mm1_pass(1, rt, a, acc)
-            expo(1, rt, acc)
+                first_product(1, rt, a, acc)
+            exponential(1, rt, acc)
             if rt == 1:
                 place(2, 0, 1)
         add_comp(4)
         add_comp(5)
         place(2, 1, 3)
-        root(4)
-        finish_h(4)
-        add_comp(6)
-        add_comp(7)
-        place(3, 0, 6, (4, 0))
-        root(5)
-        finish_h(5)
-        place(3, 1, 7, (5, 0))
-        place(4, 0, 5, (5, 1))
-        root(6)
-        finish_h(6)
-        place(4, 1, 0, (6, 0))
-        place(5, 0, 1, (6, 1))
-        root(7)
-        finish_h(7)
-        place(5, 1, 2, (7, 0))
-        place(6, 0, 3, (7, 1))
-        place(6, 1, 4)
-        place(7, 0, 5)
-        place(7, 1, 6)
-        finish_out(N_TILES - 2)
-        finish_out(N_TILES - 1, 2)
+        make_h(4)
+        quantize_h(4)
+        place(3, 0, 6, behind=(4, 0))
+        make_h(5)
+        quantize_h(5)
+        place(3, 1, 7, behind=(5, 0))
+        place(4, 0, 5, behind=(5, 1))
+        add_comp_by_transposes(6, there=(6, 3), back=(0, 2))
+        make_h(6)
+        quantize_h(6)
+        place(4, 1, 0, behind=(6, 0))
+        place(5, 0, 2, behind=(6, 1))
+        add_comp_by_transposes(7, there=(7, 5), back=(4, 1))
+        make_h(7)
+        quantize_h(7)
+        place(5, 1, 4, behind=(7, 0))
+        place(6, 0, 1, behind=(7, 1))
+        place(6, 1, 6)
+        place(7, 0, 3)
+        place(7, 1, 7)
+        finish(N_TILES - 2)
+        finish(N_TILES - 1, stores=2)

from contextlib import ExitStack

import concourse.mybir as mybir
from concourse.masks import make_identity

K, H, N, T, S = 1536, 1024, 768, 4096, 1024
FLOPS = 2 * K * H * S + 2 * H * N * S

F32 = mybir.dt.float32
BF16 = mybir.dt.bfloat16
I32 = mybir.dt.int32
U32 = mybir.dt.uint32
U16 = mybir.dt.uint16
U8 = mybir.dt.uint8
FP8X4 = mybir.dt.float8_e4m3fn_x4
FP4X4 = mybir.dt.float4_e2m1fn_x4
ACT = mybir.ActivationFunctionType
ALU = mybir.AluOpType

P = 128
PACK = 4
PASS = P * PACK
BANK = 512
K_PASSES = K // PASS
R_PASSES = H // PASS
R_TILES = H // P
N_TILES = N // P
HALF = 512
QUARTER = 256
PIECE = 128
PIECES = S // PIECE
PIECES_PER_HALF = HALF // PIECE
PART_TILES = 3
PART_COLS = PART_TILES * P
LIST_ROWS = 16
SCALE_ROWS = 16
QUADRANT = 32
QUADRANT_ROWS = 4
STAGED_ROW0 = 16
STAGED_ROWS = SCALE_ROWS * K_PASSES
LINE = 4
W2_WORD_RUNS = ((0, 256), (256, 768))


def tile_list_fraction_loading_kernel(
    tc, tab_words, tab_scales, offs, w1_words, w1_scales, comp, cap, w2, offs2, wgo, x0, out
):
    nc = tc.nc
    with ExitStack() as ctx:
        keep = ctx.enter_context(tc.tile_pool(name="keep", bufs=1))
        ring = ctx.enter_context(tc.tile_pool(name="ring", bufs=2))
        psum = ctx.enter_context(tc.psum_pool(name="psum", bufs=1))

        def bank(number):
            return psum.tile([P, BANK], F32, name="bank%d" % number, tag="bank%d" % number)

        def big_tile(pool, number, shape, dtype):
            return pool.tile(shape, dtype, name="big%d" % number, tag="big%d" % number, bufs=1)

        idx = keep.tile([P, S // LIST_ROWS], U16, name="idx")
        idx2 = keep.tile([P, S // LIST_ROWS], U16, name="idx2")
        w1_words_in = ring.tile([P, K_PASSES, H], U16, name="w1_words_in", tag="work", bufs=1)
        w1_scales_in = ring.tile([P, K_PASSES, H], U8, name="w1_scales_in", tag="w2_bf16", bufs=1, align_bytes=64)
        cap_sb = keep.tile([P, R_PASSES, PACK], F32, name="cap_sb")
        v_scales = keep.tile([P, K_PASSES, S], U8, name="v_scales", align_bytes=64)
        picked_scales = keep.tile([P, S], U8, name="picked_scales")
        table = []

        def load_table(pool, a):
            table.append(big_tile(pool, a, [P, T], U32))
            nc.sync.dma_start(table[a][:].bitcast(I32), tab_words[a].rearrange("p c i -> p (c i)").bitcast(I32))

        with tc.tile_pool(name="early", bufs=1) as early:
            staged_scales = early.tile([P, T], U8, name="staged_scales")
            nc.vector.memset(w1_scales_in[:].bitcast(I32), 0)
            nc.vector.memset(staged_scales[0:STAGED_ROW0, :].bitcast(I32), 0)
            nc.vector.memset(staged_scales[STAGED_ROW0 + STAGED_ROWS : P, :].bitcast(I32), 0)
            nc.vector.memset(v_scales[:].bitcast(I32), 0)

            nc.sync.dma_start(idx[:], offs)
            nc.sync.dma_start(
                staged_scales[STAGED_ROW0 : STAGED_ROW0 + STAGED_ROWS, :].bitcast(I32),
                tab_scales.rearrange("a q c -> q a c").bitcast(I32),
            )
            nc.sync.dma_start(idx2[:], offs2)
            nc.sync.dma_start(w1_words_in[:].bitcast(I32), w1_words.rearrange("a p c -> p a c").bitcast(I32))
            for quad in range(P // QUADRANT):
                rows = slice(QUADRANT_ROWS * quad, QUADRANT_ROWS * (quad + 1))
                nc.sync.dma_start(
                    w1_scales_in[QUADRANT * quad : QUADRANT * quad + QUADRANT_ROWS, :, :].bitcast(I32),
                    w1_scales[:, rows, :].rearrange("a q c -> q a c").bitcast(I32),
                )
            load_table(ring, 0)
            nc.gpsimd.dma_start(cap_sb[:], cap.rearrange("(g p t) -> p g t", p=P, t=PACK))
            nc.vector.tensor_copy(picked_scales[:], staged_scales[:].indirect(idx[:]))

        late = ctx.enter_context(tc.tile_pool(name="late", bufs=1))
        for quad in range(P // QUADRANT):
            row0 = STAGED_ROW0 + QUADRANT_ROWS * K_PASSES * quad
            queue = nc.sync if quad % 2 == 0 else nc.scalar
            queue.dma_start(
                v_scales[QUADRANT * quad : QUADRANT * quad + QUADRANT_ROWS, :, :].bitcast(I32),
                picked_scales[row0 : row0 + QUADRANT_ROWS * K_PASSES, :].bitcast(I32),
            )
        for a in range(1, K_PASSES):
            load_table(late, a)

        comp_sb = {}
        w2_in = {}
        wgo_sb = [late.tile([P, HALF], F32, name="wgo%d" % half) for half in range(S // HALF)]

        def load_comp(first, width):
            for g in range(R_PASSES):
                rows = late.tile([P, PACK, width], F32, name="comp%d_%d" % (first, g))
                nc.sync.dma_start(
                    rows[:],
                    comp[g * PASS : (g + 1) * PASS, first : first + width].rearrange("(p t) j -> p t j", t=PACK),
                )
                for j in range(0, width, PIECE):
                    comp_sb[(first + j) // PIECE, g] = rows[:, :, j : j + PIECE]

        def load_w2(part):
            cols = slice(part * PART_COLS, (part + 1) * PART_COLS)
            for g in range(R_PASSES):
                w2_in[part, g] = late.tile([P, PACK, PART_COLS], F32, name="w2_in%d_%d" % (part, g))
                nc.sync.dma_start(
                    w2_in[part, g][:], w2[g * PASS : (g + 1) * PASS, cols].rearrange("(p t) n -> p t n", t=PACK)
                )

        load_comp(0, QUARTER)
        load_w2(0)
        nc.sync.dma_start(wgo_sb[0][:], wgo[:, :HALF])
        load_comp(QUARTER, QUARTER)
        load_w2(1)
        load_comp(HALF, HALF)
        nc.sync.dma_start(wgo_sb[1][:], wgo[:, HALF:])

        log_cap = keep.tile([P, R_TILES], F32, name="log_cap")
        inv_cap = keep.tile([P, R_TILES], F32, name="inv_cap")
        nc.scalar.activation(log_cap[:], cap_sb[:].rearrange("p g t -> p (g t)"), ACT.Ln)
        nc.scalar.activation(inv_cap[:], log_cap[:], ACT.Exp, scale=-1.0)
        ident = keep.tile([P, P], F32, name="ident")
        make_identity(nc, ident[:])

        w1_codes = keep.tile([P, K_PASSES * H], U16, name="w1_codes", align_bytes=64)
        w1_planes = keep.tile([P, K_PASSES * H], U8, name="w1_planes", align_bytes=64)
        for ordered, arrived in ((w1_codes, w1_words_in), (w1_planes, w1_scales_in)):
            nc.vector.tensor_copy(
                ordered[:].rearrange("p (b t m) -> p b t m", t=PACK, m=P),
                arrived[:].rearrange("p a (g m t) -> p (a g) t m", t=PACK, m=P),
            )

        v_codes = {}
        for a in range(K_PASSES - 1):
            whole = keep.tile([P, S], U32, name="v_codes%d" % a, align_bytes=64)
            nc.vector.tensor_copy(whole[:], table[a][:].indirect(idx[:]))
            for half in range(S // HALF):
                v_codes[a, half] = whole[:, half * HALF : (half + 1) * HALF]
        last = K_PASSES - 1
        for half in range(S // HALF):
            picked = keep.tile([P, HALF], U32, name="v_codes%d_%d" % (last, half), align_bytes=64)
            entries = idx[:, half * HALF // LIST_ROWS : (half + 1) * HALF // LIST_ROWS]
            nc.vector.tensor_copy(picked[:], table[last][:].indirect(entries))
            v_codes[last, half] = picked[:]

        x_sb = []
        for pair in range(N_TILES // 2):
            both = big_tile(ring if pair == 0 else late, pair, [P, 2, S], F32)
            nc.sync.dma_start(both[:], x0[2 * pair * P : (2 * pair + 2) * P, :].rearrange("(c p) m -> p c m", p=P))
            x_sb.extend([both[:, 0, :], both[:, 1, :]])

        work = []
        denominators = {}
        roots = {}
        h_mx = {}
        w2_mx = []
        pages = [keep.tile([P, S], F32, name="page%d" % nt) for nt in range(N_TILES)]

        def first_product(half, rt, a, acc):
            cols = slice(a * H + rt * P, a * H + (rt + 1) * P)
            nc.tensor.matmul_mx(
                out=acc[:],
                lhsT=w1_codes[:, cols].bitcast(FP4X4),
                lhsT_scale=w1_planes[:, cols],
                rhs=v_codes[a, half].bitcast(FP8X4),
                rhs_scale=v_scales[:, a, half * HALF : (half + 1) * HALF],
                start=(a == 0),
                stop=(a == K_PASSES - 1),
            )

        def open_half():
            work.append(ring.tile([P, PIECES_PER_HALF, R_TILES, PIECE], F32, name="work", tag="work", bufs=1))

        def exponential(half, rt, acc):
            nc.scalar.activation(work[half][:, :, rt, :], acc[:].rearrange("p (s j) -> p s j", j=PIECE), ACT.Exp)

        def exponentials_of(piece, g):
            half, within = divmod(piece, PIECES_PER_HALF)
            return work[half][:, within, g * PACK : (g + 1) * PACK, :]

        def add_comp(piece):
            for g in range(R_PASSES):
                values = exponentials_of(piece, g)
                nc.vector.tensor_tensor(values, values, comp_sb[piece, g], ALU.add)
                denominators[piece, g] = values

        def add_comp_by_transposes(piece, there, back):
            for g in range(R_PASSES):
                values = exponentials_of(piece, g)
                acc = bank(there[g])
                for t in range(PACK):
                    turned = acc[:, t * P : (t + 1) * P]
                    nc.tensor.matmul(
                        turned, comp_sb[piece, g][:, t, :], ident[:], start=True, stop=False, is_transpose=True
                    )
                    nc.tensor.matmul(turned, values[:, t, :], ident[:], start=False, stop=True, is_transpose=True)
                nc.scalar.copy(values, acc[:].rearrange("j (t p) -> j t p", t=PACK))
            for g in range(R_PASSES):
                values = exponentials_of(piece, g)
                acc = bank(back[g])
                for t in range(PACK):
                    nc.tensor.transpose(acc[:, t * PIECE : (t + 1) * PIECE], values[:, t, :], ident[:])
                denominators[piece, g] = acc[:].rearrange("p (t j) -> p t j", t=PACK)

        def root_buffer(piece, g, width):
            name = "root%d_%d" % (piece % PIECES_PER_HALF, g)
            return ring.tile([P, width], F32, name=name, tag=name, bufs=1)

        def make_h(piece):
            for g in range(R_PASSES):
                roots[piece, g] = root_buffer(piece, g, PACK * PIECE)
                for t in range(PACK):
                    rt = g * PACK + t
                    nc.scalar.activation(
                        roots[piece, g][:, t * PIECE : (t + 1) * PIECE],
                        denominators[piece, g][:, t, :],
                        ACT.Abs_reciprocal_sqrt,
                        scale=inv_cap[:, rt : rt + 1],
                    )

        def quantize_h(piece):
            h_bf16 = ring.tile([P, R_PASSES * PIECE * PACK], BF16, name="h_bf16", tag="h_bf16", align_bytes=64)
            for g in range(R_PASSES):
                nc.scalar.activation(
                    h_bf16[:, g * PIECE * PACK : (g + 1) * PIECE * PACK].rearrange(
                        "p (c i t) -> p c t i", i=LINE, t=PACK
                    ),
                    roots[piece, g][:].rearrange("p (t c i) -> p c t i", i=LINE, t=PACK),
                    ACT.Square,
                )
            codes = ring.tile([P, R_PASSES * PIECE], U32, name="h_codes", tag="h_codes", bufs=4, align_bytes=64)
            scales = ring.tile([P, R_PASSES * PIECE], U8, name="h_scales", tag="h_scales", bufs=4, align_bytes=64)
            nc.vector.quantize_mx(out=codes[:].bitcast(FP8X4), scales=scales[:], in_=h_bf16[:])
            h_mx[piece] = (codes, scales)

        def quantize_w2(part):
            width = PART_COLS * PACK
            w2_bf16 = ring.tile([P, R_PASSES * width], BF16, name="w2_bf16", tag="w2_bf16", bufs=1, align_bytes=64)
            for g in range(R_PASSES):
                nc.vector.tensor_copy(
                    w2_bf16[:, g * width : (g + 1) * width].rearrange("p (c i t) -> p c t i", i=LINE, t=PACK),
                    w2_in[part, g][:].rearrange("p t (c i) -> p c t i", i=LINE),
                )
            codes = keep.tile([P, R_PASSES * PART_COLS], U32, name="w2_codes%d" % part, align_bytes=64)
            scales = keep.tile([P, R_PASSES * PART_COLS], U8, name="w2_scales%d" % part, align_bytes=64)
            for lo, hi in W2_WORD_RUNS:
                nc.vector.quantize_mx(
                    out=codes[:, lo:hi].bitcast(FP8X4), scales=scales[:, lo:hi], in_=w2_bf16[:, PACK * lo : PACK * hi]
                )
            w2_mx.append((codes, scales))

        def finish(nt, stores=1):
            for i in range(stores):
                cols = slice(i * S // stores, (i + 1) * S // stores)
                gain = ring.tile([P, S // stores], F32, name="gain", tag="gain")
                nc.scalar.activation(gain[:], pages[nt][:, cols], ACT.Identity, bias=1.0)
                nc.vector.tensor_tensor(x_sb[nt][:, cols], gain[:], x_sb[nt][:, cols], ALU.mult)
                nc.sync.dma_start(out[nt * P : (nt + 1) * P, cols], x_sb[nt][:, cols])

        def place(piece, part, number, behind=None):
            h_codes, h_scales = h_mx[piece]
            w2_codes, w2_scales = w2_mx[part]
            acc = bank(number)
            for i in range(PART_TILES):
                for g in range(R_PASSES):
                    cols = slice(g * PART_COLS + i * P, g * PART_COLS + (i + 1) * P)
                    nc.tensor.matmul_mx(
                        out=acc[:, i * PIECE : (i + 1) * PIECE],
                        lhsT=w2_codes[:, cols].bitcast(FP8X4),
                        lhsT_scale=w2_scales[:, cols],
                        rhs=h_codes[:, g * PIECE : (g + 1) * PIECE].bitcast(FP8X4),
                        rhs_scale=h_scales[:, g * PIECE : (g + 1) * PIECE],
                        start=(g == 0),
                        stop=(g == R_PASSES - 1),
                    )
            if behind is None:
                y = ring.tile([P, PART_TILES * PIECE], F32, name="y", tag="y", bufs=4)
            else:
                y = root_buffer(behind[0], behind[1], PART_TILES * PIECE)
            nc.scalar.copy(y[:], acc[:, : PART_TILES * PIECE])
            half, within = divmod(piece, PIECES_PER_HALF)
            places = idx2[:, piece * PIECE // LIST_ROWS : (piece + 1) * PIECE // LIST_ROWS]
            for i in range(PART_TILES):
                nt = part * PART_TILES + i
                nc.vector.tensor_tensor(
                    pages[nt][:].indirect(places),
                    y[:, i * PIECE : (i + 1) * PIECE],
                    wgo_sb[half][:, within * PIECE : (within + 1) * PIECE],
                    ALU.mult,
                )
                if piece == PIECES - 1 and nt >= 2:
                    finish(nt - 2)


        accs = [bank(rt) for rt in range(R_TILES)]
        for a in range(K_PASSES):
            for rt in range(R_TILES):
                first_product(0, rt, a, accs[rt])
        open_half()
        for rt in range(R_TILES):
            exponential(0, rt, accs[rt])
        quantize_w2(0)
        add_comp(0)
        make_h(0)
        quantize_h(0)
        add_comp(1)
        make_h(1)
        place(0, 0, 5)
        quantize_h(1)
        add_comp(2)
        add_comp(3)
        quantize_w2(1)
        make_h(2)
        quantize_h(2)
        place(1, 0, 6, behind=(2, 0))
        make_h(3)
        quantize_h(3)
        place(0, 1, 7, behind=(3, 0))
        place(1, 1, 5, behind=(3, 1))

        open_half()
        for rt, number in enumerate((0, 1, 2, 3, 4, 0, 2, 3)):
            acc = bank(number)
            for a in range(K_PASSES):
                first_product(1, rt, a, acc)
            exponential(1, rt, acc)
            if rt == 1:
                place(2, 0, 1)
        add_comp(4)
        add_comp(5)
        place(2, 1, 3)
        make_h(4)
        quantize_h(4)
        place(3, 0, 6, behind=(4, 0))
        make_h(5)
        quantize_h(5)
        place(3, 1, 7, behind=(5, 0))
        place(4, 0, 5, behind=(5, 1))
        add_comp_by_transposes(6, there=(6, 3), back=(0, 2))
        make_h(6)
        quantize_h(6)
        place(4, 1, 0, behind=(6, 0))
        place(5, 0, 2, behind=(6, 1))
        add_comp_by_transposes(7, there=(7, 5), back=(4, 1))
        make_h(7)
        quantize_h(7)
        place(5, 1, 4, behind=(7, 0))
        place(6, 0, 1, behind=(7, 1))
        place(6, 1, 6)
        place(7, 0, 3)
        place(7, 1, 7)
        finish(N_TILES - 2)
        finish(N_TILES - 1, stores=2)
